import numpy as np
import ml_dtypes


def mxq(x, axis, fmt="e4m3"):
    dtype, down = {"e4m3": (ml_dtypes.float8_e4m3fn, 7), "e5m2": (ml_dtypes.float8_e5m2, 14)}[fmt]
    v = np.moveaxis(np.asarray(x, np.float32).astype(ml_dtypes.bfloat16).astype(np.float64), axis, -1)
    blocks = v.reshape(v.shape[:-1] + (-1, 32))
    amax = np.abs(blocks).max(-1, keepdims=True)
    byte = np.maximum(np.where(amax > 0, np.frexp(amax)[1] - 1 + 127, 0) - down, 1)
    scale = np.exp2(byte - 127.0)
    codes = (blocks / scale).astype(np.float32).astype(dtype).astype(np.float64)
    return np.moveaxis((codes * scale).reshape(v.shape), -1, axis)


WIDE = False


def mx_kscale(k):
    if not WIDE:
        return np.ones(k)
    levels = np.array([10, -10, 5, -5, 0])
    if k % 512:
        return np.exp2(np.random.permutation(np.resize(levels, k // 32))).repeat(32)
    a = np.empty((k // 512, 16))
    for p in range(k // 512):
        a[p, :8] = np.random.permutation(np.resize(levels, 8))
        for g in range(8):
            far = levels[np.abs(levels - a[p, g]) >= 10]
            a[p, g + 8] = far[np.random.randint(len(far))]
    return np.exp2(a.ravel()).repeat(32)


BF16 = ml_dtypes.bfloat16


def bf(x):
    return np.asarray(x, np.float32).astype(BF16)


def f64(x):
    return np.asarray(x).astype(np.float64)


E2M1 = np.array([0.0, 0.5, 1.0, 1.5, 2.0, 3.0, 4.0, 6.0, -0.0, -0.5, -1.0, -1.5, -2.0, -3.0, -4.0, -6.0])


def pack_weight(w, fmt):
    k, n = w.shape
    w = f64(bf(w)).reshape(k // 32, 32, n)
    amax = np.abs(w).max(1)
    if fmt == "e4m3":
        byte = np.frexp(amax)[1] - 1 + 127 - 7
    else:
        mant, ex = np.frexp(amax / 6.0)
        byte = np.where(mant > 0.5, ex, ex - 1) + 127
    byte = np.clip(np.where(amax > 0, byte, 1), 1, 254)
    scaled = (w * np.exp2(127.0 - byte)[:, None, :]).reshape(k, n).astype(np.float32)
    by_word = np.ascontiguousarray(scaled.reshape(k // 512, 128, 4, n).transpose(0, 1, 3, 2))
    if fmt == "e4m3":
        words = by_word.astype(ml_dtypes.float8_e4m3fn).view(np.uint8)
    else:
        c = by_word.astype(ml_dtypes.float4_e2m1fn).view(np.uint8) & 0xF
        words = c[..., 0::2] | (c[..., 1::2] << 4)
    return np.ascontiguousarray(words), np.ascontiguousarray(byte.astype(np.uint8).reshape(k // 512, 16, n))


def unpack_weight(words, scales, fmt):
    g, p, n, _ = words.shape
    if fmt == "e4m3":
        vals = np.ascontiguousarray(words).view(ml_dtypes.float8_e4m3fn).astype(np.float64)
    else:
        nib = np.empty((g, p, n, 4), np.uint8)
        nib[..., 0::2] = words & 0xF
        nib[..., 1::2] = words >> 4
        vals = E2M1[nib]
    vals = vals * np.repeat(np.exp2(scales.astype(np.float64) - 127.0), 8, axis=1)[..., None]
    return vals.transpose(0, 1, 3, 2).reshape(g * 512, n)
def pack4(w):
    words, scales = pack_weight(w, "e2m1")
    return words.reshape(words.shape[0], 128, -1), scales


def unpack4(words, scales):
    return unpack_weight(words.reshape(words.shape[0], 128, -1, 2), scales, "e2m1")


N, D, F, O, T = 1024, 1024, 1024, 512, 3


def normalized_hermite(u):
    u2 = u * u
    u3 = u2 * u
    h1 = u
    h2 = (u2 - 1.0) / np.sqrt(2.0)
    h3 = (u3 - 3.0 * u) / np.sqrt(6.0)
    return h1, h2, h3


def draw0():
    s = mx_kscale(D)
    t = np.stack([mx_kscale(F) for _ in range(T)])
    x = bf(np.random.standard_normal((N, D)) * s)
    words, scales = pack4(np.random.standard_normal((D, F)) / np.sqrt(D) / s[:, None])
    return {"x": x,
            "w_words": words,
            "w_scales": scales,
            "g": bf((1.0 + 0.1 * np.random.standard_normal((T, F))) * t),
            "c": bf(np.random.standard_normal((T, F, O)) / np.sqrt(F) / t[:, :, None]),
            "b": bf(np.random.standard_normal(O) * 0.5)}


def core(x, w_words, w_scales, g, c, b):
    g, c = f64(g), f64(c)
    u = mxq(f64(x), 1, "e4m3") @ unpack4(w_words, w_scales)
    h1, h2, h3 = normalized_hermite(u)
    k1 = h1 * g[0]
    k2 = h2 * g[1]
    k3 = h3 * g[2]
    y1 = mxq(k1, 1, "e4m3") @ mxq(c[0], 0, "e4m3")
    y2 = mxq(k2, 1, "e4m3") @ mxq(c[1], 0, "e4m3")
    y3 = mxq(k3, 1, "e4m3") @ mxq(c[2], 0, "e4m3")
    return y1 + y2 + y3 + f64(b)


def e4m3fn_bytes(y):
    return np.clip(np.asarray(y, np.float64), -448.0, 448.0).astype(np.float32).astype(ml_dtypes.float8_e4m3fn).view(np.uint8)


def e4m3fn_values(b):
    return np.asarray(b, np.uint8).view(ml_dtypes.float8_e4m3fn).astype(np.float64)


def setup_inputs():
    d = draw0()
    x0 = np.asarray(d['x']).astype(np.float64)
    s = (np.max(np.abs(x0), axis=(0,), keepdims=True) / 448.0).astype(np.float32)
    out = {}
    for k, v in d.items():
        if k == 'x':
            out['x_bytes'] = e4m3fn_bytes(x0 / s.astype(np.float64))
            out['x_scale'] = s
        else:
            out[k] = v
    return out


def reference(x_bytes, x_scale, w_words, w_scales, g, c, b):
    return core(e4m3fn_values(x_bytes) * x_scale.astype(np.float64), w_words, w_scales, g, c, b)

@@ -1,0 +1,464 @@
+import math
+from contextlib import ExitStack
+
+import concourse.mybir as mybir
+from concourse.masks import make_identity
+
+N, D, F, O, T = 1024, 1024, 1024, 512, 3
+FLOPS = 2 * N * D * F + T * 2 * N * F * O
+
+F32 = mybir.dt.float32
+BF16 = mybir.dt.bfloat16
+I32 = mybir.dt.int32
+U32 = mybir.dt.uint32
+U8 = mybir.dt.uint8
+FP8 = mybir.dt.float8_e4m3fn
+FP8X4 = mybir.dt.float8_e4m3fn_x4
+FP4X4 = mybir.dt.float4_e2m1fn_x4
+ALU = mybir.AluOpType
+ACT = mybir.ActivationFunctionType
+
+P = 128
+PACK = 4
+K_PASS = P * PACK
+D_PASSES = D // K_PASS
+F_PASSES = F // K_PASS
+ROW_TILES = N // P
+CHUNK = 2 * P
+STEPS = (N // CHUNK) * F_PASSES
+RUN = 8
+
+
+def tile_hermitechaosridgeexpansiondegreethree_w4_kernel(
+    tc, x_bytes, x_scale, w_words, w_scales, g, c, b, out
+):
+    nc = tc.nc
+    with ExitStack() as ctx:
+        keep = ctx.enter_context(tc.tile_pool(name="keep", bufs=1))
+        work = ctx.enter_context(tc.tile_pool(name="work", bufs=2))
+        psum = ctx.enter_context(tc.psum_pool(name="psum", bufs=1))
+        ctx.enter_context(tc.manual_schedule())
+
+        ident = keep.tile([P, P], F32, name="ident")
+        make_identity(nc, ident[:])
+        ws_raw = keep.tile([P, D_PASSES * F // 4], I32, name="ws_raw")
+        nc.gpsimd.memset(ws_raw[:], 0)
+        for quad in range(4):
+            nc.gpsimd.dma_start(
+                out=ws_raw[32 * quad : 32 * quad + 4, :].rearrange("r (k n) -> r k n", k=D_PASSES),
+                in_=w_scales[:, 4 * quad : 4 * quad + 4, :].rearrange("k r n -> r k n").bitcast(I32),
+            )
+        g_rows = keep.tile([P, PACK, P], F32, name="g_rows")
+        nc.vector.memset(g_rows[:], 0.0)
+
+        xs_col = keep.tile([P, D_PASSES, PACK], F32, name="xs_col")
+        nc.sync.dma_start(out=xs_col[:], in_=x_scale.rearrange("o (k p j) -> p (o k) j", p=P, j=PACK))
+        x_raw = []
+
+        def load_x(i):
+            xr = keep.tile([P, D], U8, name="x_raw%d" % i)
+            nc.sync.dma_start(out=xr[:], in_=x_bytes[i * P : (i + 1) * P, :])
+            x_raw.append(xr)
+
+        c_raw = {}
+
+        def load_c(m):
+            d, gf = divmod(m, F_PASSES)
+            cr = keep.tile([P, PACK, O], BF16, name="c_raw%d" % m)
+            rows = c[d, gf * K_PASS : (gf + 1) * K_PASS, :].rearrange("(q t r) o -> t q r o", t=PACK, r=RUN)
+            for t in range(PACK):
+                nc.sync.dma_start(out=cr[:, t, :], in_=rows[t])
+            c_raw[m] = cr
+
+        load_x(0)
+        w_raw = []
+        for gk in range(D_PASSES):
+            wr = keep.tile([P, F // 2], I32, name="w_raw%d" % gk)
+            nc.sync.dma_start(out=wr[:], in_=w_words[gk].bitcast(I32))
+            w_raw.append(wr)
+        load_x(1)
+        load_c(0)
+        g_raw = keep.tile([T * F_PASSES, K_PASS], BF16, name="g_raw")
+        nc.sync.dma_start(out=g_raw[:], in_=g.rearrange("d (h f) -> (d h) f", h=F_PASSES))
+        load_x(2)
+        load_x(3)
+        load_c(1)
+        load_c(2)
+        load_x(4)
+        load_x(5)
+        load_c(3)
+        load_x(6)
+        load_x(7)
+        load_c(4)
+        load_c(5)
+        bias = keep.tile([P, O], BF16, name="bias")
+        nc.sync.dma_start(out=bias[:], in_=b.partition_broadcast(P))
+
+        xs_all = keep.tile([P, D], F32, name="xs_all")
+        for gk in range(D_PASSES):
+            bank = psum.tile([P, PACK, P], F32, name="turn", tag="turn%d" % gk)
+            for j in range(PACK):
+                nc.tensor.transpose(bank[:, j, :], xs_col[:, gk, j : j + 1].to_broadcast([P, P]), ident[:])
+            nc.scalar.activation(
+                out=xs_all[:, gk * K_PASS : (gk + 1) * K_PASS].rearrange("r (p j) -> r p j", j=PACK),
+                in_=bank[:].rearrange("r j p -> r p j"),
+                func=ACT.Identity,
+            )
+
+        gains = {}
+
+        def turn_gains():
+            nc.vector.tensor_copy(
+                out=g_rows[0 : T * F_PASSES].rearrange("m t (q r) -> m t q r", r=RUN),
+                in_=g_raw[:].rearrange("m (q t r) -> m t q r", t=PACK, r=RUN),
+            )
+            g_bank = psum.tile([P, PACK, P], F32, name="g_bank", tag="acc0")
+            for t in range(PACK):
+                nc.tensor.transpose(g_bank[:, t, :], g_rows[:, t, :], ident[:])
+            gains["bank"] = g_bank
+
+        def gain(name, d, factor):
+            col = keep.tile([P, F_PASSES, PACK], F32, name=name)
+            src = gains["bank"][:, :, d * F_PASSES : (d + 1) * F_PASSES].rearrange("p t h -> p h t")
+            nc.scalar.activation(out=col[:], in_=src, func=ACT.Copy, scale=factor)
+            gains[name] = col
+
+        def scale_gains():
+            gain("g1", 0, 1.0)
+            gain("g3_mul", 2, 1.0 / math.sqrt(6.0))
+            gain("g3_add", 2, -3.0 / math.sqrt(6.0))
+            gain("g2_mul", 1, 1.0 / math.sqrt(2.0))
+            gain("g2_add", 1, -1.0 / math.sqrt(2.0))
+
+        w_codes, w_planes = [], []
+
+        def order_w(gk):
+            wc = keep.tile([P, 2 * F], U8, name="w_codes%d" % gk, align_bytes=64)
+            nc.vector.tensor_copy(
+                out=wc[:].bitcast(I32).rearrange("p (h t q w) -> p h t q w", h=F_PASSES, t=PACK, w=4),
+                in_=w_raw[gk][:].rearrange("p (h q t w) -> p h t q w", h=F_PASSES, t=PACK, w=4),
+            )
+            w_codes.append(wc)
+
+        def order_w_scales():
+            wp = keep.tile([P, D_PASSES * F], U8, name="w_plane", align_bytes=64)
+            nc.vector.tensor_copy(
+                out=wp[:].bitcast(I32).rearrange("p (h t q w) -> p h t q w", t=PACK, q=16, w=2),
+                in_=ws_raw[:].rearrange("p (h q t w) -> p h t q w", t=PACK, q=16, w=2),
+            )
+            w_planes.append(wp)
+
+        x_wide, x_grouped, x_codes, x_planes = {}, {}, {}, {}
+
+        def widen_x(i):
+            xw = work.tile([P, D], BF16, name="x_wide", bufs=3)
+            width = K_PASS if i == 0 else D
+            for start in range(0, D, width):
+                cols = slice(start, start + width)
+                nc.vector.tensor_tensor(
+                    out=xw[:, cols], in0=x_raw[i][:, cols].bitcast(FP8), in1=xs_all[:, cols], op=ALU.mult
+                )
+            x_wide[i] = xw
+
+        def turn_x(i):
+            words = x_wide[i][:].bitcast(F32)
+            bank = psum.tile([P, D_PASSES, 2, P], F32, name="turn", tag="turn%d" % (i % 2))
+            for gk in range(D_PASSES):
+                for u in range(2):
+                    nc.tensor.transpose(bank[:, gk, u, :], words[:, 256 * gk + u : 256 * (gk + 1) : 2], ident[:])
+            x_grouped[i] = bank
+
+        def empty_x(i):
+            xg = work.tile([P, D_PASSES * P * PACK], BF16, name="x_grouped", bufs=3, align_bytes=64)
+            nc.scalar.copy(
+                out=xg[:].bitcast(F32).rearrange("p (k r u) -> p k r u", k=D_PASSES, u=2),
+                in_=x_grouped[i][:].rearrange("p k u r -> p k r u"),
+            )
+            x_grouped[i] = xg
+
+        def quantize(name, src):
+            width = src.shape[1] // PACK
+            codes = keep.tile([P, width], U32, name=name + "_codes", align_bytes=64)
+            plane = keep.tile([P, width], U8, name=name + "_plane", align_bytes=64)
+            nc.vector.quantize_mx(out=codes[:].bitcast(FP8X4), scales=plane[:], in_=src)
+            return codes, plane
+
+        def quantize_x(i):
+            x_codes[i], x_planes[i] = quantize("x%d" % i, x_grouped[i][:])
+
+        u_banks = {}
+
+        def project(s, h):
+            j, gf = divmod(s, F_PASSES)
+            i = 2 * j + h
+            bank = psum.tile([P, PACK, P], F32, name="u", tag="u%d" % ((2 * s + h) % 4))
+            for t in range(PACK):
+                col = (gf * PACK + t) * P
+                for gk in range(D_PASSES):
+                    nc.tensor.matmul_mx(
+                        out=bank[:, t, :],
+                        lhsT=w_codes[gk][:, 2 * col : 2 * (col + P)].bitcast(FP4X4),
+                        lhsT_scale=w_planes[0][:, gk * F + col : gk * F + col + P],
+                        rhs=x_codes[i][:, gk * P : (gk + 1) * P].bitcast(FP8X4),
+                        rhs_scale=x_planes[i][:, gk * P : (gk + 1) * P],
+                        start=(gk == 0),
+                        stop=(gk == D_PASSES - 1),
+                    )
+            u_banks[s, h] = bank
+
+        squares, cubic_factor, k2_rows = {}, {}, {}
+
+        def square(s, h):
+            if h == 0:
+                squares[s] = work.tile([P, PACK, CHUNK], F32, name="square")
+            nc.scalar.activation(out=squares[s][:, :, h * P : (h + 1) * P], in_=u_banks[s, h][:], func=ACT.Square)
+
+        def affine(s, dst, mul, add):
+            gf = s % F_PASSES
+            for t in range(PACK):
+                nc.scalar.activation(
+                    out=dst[:, t, :],
+                    in_=squares[s][:, t, :],
+                    func=ACT.Identity,
+                    scale=mul[:, gf, t : t + 1],
+                    bias=add[:, gf, t : t + 1],
+                )
+
+        def scalar_part(s):
+            square(s, 0)
+            square(s, 1)
+            cubic_factor[s] = work.tile([P, PACK, CHUNK], F32, name="cubic_factor")
+            affine(s, cubic_factor[s], gains["g3_mul"], gains["g3_add"])
+            k2_rows[s] = work.tile([P, PACK, CHUNK], BF16, name="k2_rows")
+            affine(s, k2_rows[s], gains["g2_mul"], gains["g2_add"])
+
+        k_grouped, k_quant = {}, {}
+
+        def grouped(s, d):
+            if (s, d) not in k_grouped:
+                k_grouped[s, d] = work.tile([P, CHUNK, PACK], BF16, name="k%d_grouped" % (d + 1), align_bytes=64)
+            return k_grouped[s, d]
+
+        def make_k1(s, h):
+            gf = s % F_PASSES
+            nc.vector.tensor_tensor(
+                out=grouped(s, 0)[:, h * P : (h + 1) * P, :],
+                in0=u_banks[s, h][:].rearrange("p t n -> p n t"),
+                in1=gains["g1"][:, gf : gf + 1, :].to_broadcast([P, P, PACK]),
+                op=ALU.mult,
+            )
+
+        def make_k3(s, h):
+            cols = slice(h * P, (h + 1) * P)
+            nc.vector.tensor_tensor(
+                out=grouped(s, 2)[:, cols, :].rearrange("p (n i) t -> p n t i", i=2),
+                in0=u_banks[s, h][:].rearrange("p t (n i) -> p n t i", i=2),
+                in1=cubic_factor[s][:, :, cols].rearrange("p t (n i) -> p n t i", i=2),
+                op=ALU.mult,
+            )
+
+        def interleave(engine, dst, src):
+            dst = dst.rearrange("p (n i) t -> p n t i", i=4)
+            src = src.rearrange("p t (n i) -> p n t i", i=4)
+            if engine == "vector":
+                nc.vector.tensor_copy(out=dst, in_=src)
+            else:
+                nc.scalar.copy(out=dst, in_=src)
+
+        def make_k2(s, engine, cols=slice(0, CHUNK)):
+            interleave(engine, grouped(s, 1)[:, cols, :], k2_rows[s][:, :, cols])
+
+        def quantize_k(s, d):
+            codes, plane = quantize("k%d_%d" % (d + 1, s), k_grouped[s, d][:].rearrange("p n t -> p (n t)"))
+            for h in range(2):
+                k_quant[s, d, h] = codes[:, h * P : (h + 1) * P], plane[:, h * P : (h + 1) * P]
+
+        def quantize_k_half(s, d, h):
+            src = k_grouped[s, d][:, h * P : (h + 1) * P, :].rearrange("p n t -> p (n t)")
+            codes, plane = quantize("k%d_%d_%d" % (d + 1, s, h), src)
+            k_quant[s, d, h] = codes[:], plane[:]
+
+        c_grouped, c_quant = {}, {}
+
+        def group_c(m, engine, half):
+            if m not in c_grouped:
+                c_grouped[m] = work.tile([P, O, PACK], BF16, name="c_grouped", align_bytes=64, bufs=3)
+            cols = slice(half * O // 2, (half + 1) * O // 2)
+            interleave(engine, c_grouped[m][:, cols, :], c_raw[m][:, :, cols])
+
+        def quantize_c(m):
+            c_quant[m] = quantize("c%d" % m, c_grouped[m][:].rearrange("p o t -> p (o t)"))
+
+        out_banks = {}
+
+        def readout(i, gf, d):
+            j, h = divmod(i, 2)
+            first = gf == 0 and d == 0
+            if first:
+                out_banks[i] = psum.tile([P, O], F32, name="acc", tag="acc%d" % h)
+            k_codes, k_plane = k_quant[j * F_PASSES + gf, d, h]
+            c_codes, c_plane = c_quant[d * F_PASSES + gf]
+            nc.tensor.matmul_mx(
+                out=out_banks[i][:],
+                lhsT=k_codes.bitcast(FP8X4),
+                lhsT_scale=k_plane,
+                rhs=c_codes[:].bitcast(FP8X4),
+                rhs_scale=c_plane[:],
+                start=first,
+                stop=(gf == F_PASSES - 1 and d == 2),
+            )
+
+        def readout_tile(i):
+            for gf in range(F_PASSES):
+                for d in range(T):
+                    readout(i, gf, d)
+
+        def finish(i):
+            res = work.tile([P, O], F32, name="result", bufs=3)
+            nc.vector.tensor_tensor(out=res[:], in0=out_banks[i][:], in1=bias[:], op=ALU.add)
+            nc.sync.dma_start(out=out[i * P : (i + 1) * P, :], in_=res[:])
+
+
+        def psum_part(s):
+            for h in range(2):
+                make_k1(s, h)
+            for h in range(2):
+                make_k3(s, h)
+
+        order_w(0)
+        order_w(1)
+        widen_x(0)
+        turn_x(0)
+        group_c(0, "scalar", 0)
+        empty_x(0)
+        widen_x(1)
+        turn_x(1)
+        turn_gains()
+        group_c(0, "scalar", 1)
+        empty_x(1)
+        scale_gains()
+        order_w_scales()
+        quantize_x(0)
+        project(0, 0)
+        widen_x(2)
+        quantize_x(1)
+        project(0, 1)
+        turn_x(2)
+        project(1, 0)
+        project(1, 1)
+        widen_x(3)
+        turn_x(3)
+        quantize_c(0)
+        group_c(1, "vector", 0)
+        scalar_part(0)
+        empty_x(2)
+        empty_x(3)
+        psum_part(0)
+        scalar_part(1)
+        group_c(1, "vector", 1)
+        quantize_x(2)
+        quantize_x(3)
+        project(2, 0)
+        project(2, 1)
+        make_k2(0, "vector")
+        quantize_k(0, 0)
+        quantize_k(0, 2)
+        widen_x(4)
+        quantize_k(0, 1)
+        quantize_c(1)
+        group_c(2, "scalar", 0)
+        group_c(2, "scalar", 1)
+        psum_part(1)
+        project(3, 0)
+        project(3, 1)
+        scalar_part(2)
+        make_k2(1, "vector")
+        quantize_k(1, 0)
+        quantize_k(1, 2)
+        widen_x(5)
+        turn_x(4)
+        turn_x(5)
+        empty_x(4)
+        empty_x(5)
+        quantize_k(1, 1)
+        quantize_c(2)
+        psum_part(2)
+        scalar_part(3)
+        quantize_x(4)
+        quantize_x(5)
+        project(4, 0)
+        project(4, 1)
+        make_k2(2, "vector")
+        quantize_k(2, 0)
+        quantize_k(2, 2)
+        widen_x(6)
+        quantize_k(2, 1)
+        group_c(3, "scalar", 0)
+        group_c(3, "scalar", 1)
+        psum_part(3)
+        project(5, 0)
+        project(5, 1)
+        scalar_part(4)
+        make_k2(3, "vector")
+        quantize_k(3, 0)
+        quantize_k(3, 2)
+        widen_x(7)
+        turn_x(6)
+        turn_x(7)
+        empty_x(6)
+        empty_x(7)
+        quantize_k(3, 1)
+        quantize_c(3)
+        group_c(4, "scalar", 0)
+        group_c(4, "vector", 1)
+        psum_part(4)
+        scalar_part(5)
+        quantize_x(6)
+        quantize_x(7)
+        project(6, 0)
+        project(6, 1)
+        quantize_c(4)
+        make_k2(4, "vector")
+        group_c(5, "scalar", 0)
+        quantize_k(4, 0)
+        quantize_k(4, 2)
+        group_c(5, "vector", 1)
+        quantize_k(4, 1)
+        quantize_c(5)
+        readout_tile(0)
+        readout_tile(1)
+        psum_part(5)
+        project(7, 0)
+        project(7, 1)
+        make_k2(5, "scalar")
+        scalar_part(6)
+        finish(0)
+        readout_tile(2)
+        quantize_k(5, 0)
+        quantize_k(5, 2)
+        finish(1)
+        readout_tile(3)
+        quantize_k(5, 1)
+        psum_part(6)
+        make_k2(6, "scalar")
+        scalar_part(7)
+        finish(2)
+        readout_tile(4)
+        quantize_k(6, 0)
+        quantize_k(6, 2)
+        finish(3)
+        readout_tile(5)
+        quantize_k(6, 1)
+        for h in range(2):
+            make_k2(7, "scalar", slice(h * P, (h + 1) * P))
+        for h in range(2):
+            finish(4 + h)
+            for d in range(T):
+                readout(6 + h, 0, d)
+            make_k1(7, h)
+            make_k3(7, h)
+            for d in range(T):
+                quantize_k_half(7, d, h)
+                readout(6 + h, 1, d)
+        finish(6)
+        finish(7)

@@ -42,17 +42,10 @@ def tile_hermitechaosridgeexpansiondegreethree_w4_kernel(
         ident = keep.tile([P, P], F32, name="ident")
         make_identity(nc, ident[:])
         ws_raw = keep.tile([P, D_PASSES * F // 4], I32, name="ws_raw")
-        nc.gpsimd.memset(ws_raw[:], 0)
-        for quad in range(4):
-            nc.gpsimd.dma_start(
-                out=ws_raw[32 * quad : 32 * quad + 4, :].rearrange("r (k n) -> r k n", k=D_PASSES),
-                in_=w_scales[:, 4 * quad : 4 * quad + 4, :].rearrange("k r n -> r k n").bitcast(I32),
-            )
+        nc.vector.memset(ws_raw[:], 0)
         g_rows = keep.tile([P, PACK, P], F32, name="g_rows")
         nc.vector.memset(g_rows[:], 0.0)
 
-        xs_col = keep.tile([P, D_PASSES, PACK], F32, name="xs_col")
-        nc.sync.dma_start(out=xs_col[:], in_=x_scale.rearrange("o (k p j) -> p (o k) j", p=P, j=PACK))
         x_raw = []
 
         def load_x(i):
@@ -71,39 +64,30 @@ def tile_hermitechaosridgeexpansiondegreethree_w4_kernel(
             c_raw[m] = cr
 
         load_x(0)
+        xs_col = keep.tile([P, D_PASSES, PACK], F32, name="xs_col")
+        nc.sync.dma_start(out=xs_col[:], in_=x_scale.rearrange("o (k p j) -> p (o k) j", p=P, j=PACK))
+        load_x(1)
+        g_raw = keep.tile([T * F_PASSES, K_PASS], BF16, name="g_raw")
+        nc.sync.dma_start(out=g_raw[:], in_=g.rearrange("d (h f) -> (d h) f", h=F_PASSES))
         w_raw = []
         for gk in range(D_PASSES):
             wr = keep.tile([P, F // 2], I32, name="w_raw%d" % gk)
             nc.sync.dma_start(out=wr[:], in_=w_words[gk].bitcast(I32))
             w_raw.append(wr)
-        load_x(1)
-        load_c(0)
-        g_raw = keep.tile([T * F_PASSES, K_PASS], BF16, name="g_raw")
-        nc.sync.dma_start(out=g_raw[:], in_=g.rearrange("d (h f) -> (d h) f", h=F_PASSES))
+        for quad in range(4):
+            nc.sync.dma_start(
+                out=ws_raw[32 * quad : 32 * quad + 4, :].rearrange("r (k n) -> r k n", k=D_PASSES),
+                in_=w_scales[:, 4 * quad : 4 * quad + 4, :].rearrange("k r n -> r k n").bitcast(I32),
+            )
         load_x(2)
         load_x(3)
-        load_c(1)
-        load_c(2)
-        load_x(4)
-        load_x(5)
-        load_c(3)
-        load_x(6)
-        load_x(7)
-        load_c(4)
+        load_c(0)
+        for i in range(4, ROW_TILES):
+            load_x(i)
+            load_c(i - 3)
         load_c(5)
         bias = keep.tile([P, O], BF16, name="bias")
         nc.sync.dma_start(out=bias[:], in_=b.partition_broadcast(P))
-
-        xs_all = keep.tile([P, D], F32, name="xs_all")
-        for gk in range(D_PASSES):
-            bank = psum.tile([P, PACK, P], F32, name="turn", tag="turn%d" % gk)
-            for j in range(PACK):
-                nc.tensor.transpose(bank[:, j, :], xs_col[:, gk, j : j + 1].to_broadcast([P, P]), ident[:])
-            nc.scalar.activation(
-                out=xs_all[:, gk * K_PASS : (gk + 1) * K_PASS].rearrange("r (p j) -> r p j", j=PACK),
-                in_=bank[:].rearrange("r j p -> r p j"),
-                func=ACT.Identity,
-            )
 
         gains = {}
 
@@ -148,16 +132,14 @@ def tile_hermitechaosridgeexpansiondegreethree_w4_kernel(
             )
             w_planes.append(wp)
 
-        x_wide, x_grouped, x_codes, x_planes = {}, {}, {}, {}
+        x_wide, x_turned, x_grouped, x_codes, x_planes = {}, {}, {}, {}, {}
 
         def widen_x(i):
-            xw = work.tile([P, D], BF16, name="x_wide", bufs=3)
+            xw = work.tile([P, D], BF16, name="x_wide", bufs=4)
             width = K_PASS if i == 0 else D
             for start in range(0, D, width):
                 cols = slice(start, start + width)
-                nc.vector.tensor_tensor(
-                    out=xw[:, cols], in0=x_raw[i][:, cols].bitcast(FP8), in1=xs_all[:, cols], op=ALU.mult
-                )
+                nc.scalar.activation(out=xw[:, cols], in_=x_raw[i][:, cols].bitcast(FP8), func=ACT.Copy)
             x_wide[i] = xw
 
         def turn_x(i):
@@ -166,14 +148,17 @@ def tile_hermitechaosridgeexpansiondegreethree_w4_kernel(
             for gk in range(D_PASSES):
                 for u in range(2):
                     nc.tensor.transpose(bank[:, gk, u, :], words[:, 256 * gk + u : 256 * (gk + 1) : 2], ident[:])
-            x_grouped[i] = bank
+            x_turned[i] = bank
 
-        def empty_x(i):
-            xg = work.tile([P, D_PASSES * P * PACK], BF16, name="x_grouped", bufs=3, align_bytes=64)
-            nc.scalar.copy(
-                out=xg[:].bitcast(F32).rearrange("p (k r u) -> p k r u", k=D_PASSES, u=2),
-                in_=x_grouped[i][:].rearrange("p k u r -> p k r u"),
-            )
+        def scale_x(i):
+            xg = work.tile([P, D_PASSES, P, 2, 2], BF16, name="x_grouped", align_bytes=64)
+            for gk in range(D_PASSES):
+                nc.vector.tensor_tensor(
+                    out=xg[:, gk],
+                    in0=x_turned[i][:, gk].bitcast(BF16).rearrange("p u (r e) -> p r u e", e=2),
+                    in1=xs_col[:, gk : gk + 1, :].rearrange("p o (u e) -> p o u e", e=2).to_broadcast([P, P, 2, 2]),
+                    op=ALU.mult,
+                )
             x_grouped[i] = xg
 
         def quantize(name, src):
@@ -184,7 +169,7 @@ def tile_hermitechaosridgeexpansiondegreethree_w4_kernel(
             return codes, plane
 
         def quantize_x(i):
-            x_codes[i], x_planes[i] = quantize("x%d" % i, x_grouped[i][:])
+            x_codes[i], x_planes[i] = quantize("x%d" % i, x_grouped[i][:].rearrange("p k r u e -> p (k r u e)"))
 
         u_banks = {}
 
@@ -224,11 +209,15 @@ def tile_hermitechaosridgeexpansiondegreethree_w4_kernel(
                     bias=add[:, gf, t : t + 1],
                 )
 
-        def scalar_part(s):
+        def squares_of(s):
             square(s, 0)
             square(s, 1)
+
+        def make_cubic_factor(s):
             cubic_factor[s] = work.tile([P, PACK, CHUNK], F32, name="cubic_factor")
             affine(s, cubic_factor[s], gains["g3_mul"], gains["g3_add"])
+
+        def make_k2_rows(s):
             k2_rows[s] = work.tile([P, PACK, CHUNK], BF16, name="k2_rows")
             affine(s, k2_rows[s], gains["g2_mul"], gains["g2_add"])
 
@@ -236,7 +225,10 @@ def tile_hermitechaosridgeexpansiondegreethree_w4_kernel(
 
         def grouped(s, d):
             if (s, d) not in k_grouped:
-                k_grouped[s, d] = work.tile([P, CHUNK, PACK], BF16, name="k%d_grouped" % (d + 1), align_bytes=64)
+                if d == 1 and 4 <= s <= 6:
+                    k_grouped[s, d] = work.tile([P, CHUNK, PACK], BF16, name="k2_late", align_bytes=64, bufs=1)
+                else:
+                    k_grouped[s, d] = work.tile([P, CHUNK, PACK], BF16, name="k%d_grouped" % (d + 1), align_bytes=64)
             return k_grouped[s, d]
 
         def make_k1(s, h):
@@ -258,6 +250,10 @@ def tile_hermitechaosridgeexpansiondegreethree_w4_kernel(
             )
 
         def interleave(engine, dst, src):
+            if engine == "gpsimd":
+                src = src.rearrange("p t n -> p n t")
+                nc.gpsimd.tensor_scalar(out=dst, in0=src, scalar1=1.0, scalar2=0.0, op0=ALU.mult, op1=ALU.add)
+                return
             dst = dst.rearrange("p (n i) t -> p n t i", i=4)
             src = src.rearrange("p t (n i) -> p n t i", i=4)
             if engine == "vector":
@@ -280,11 +276,10 @@ def tile_hermitechaosridgeexpansiondegreethree_w4_kernel(
 
         c_grouped, c_quant = {}, {}
 
-        def group_c(m, engine, half):
-            if m not in c_grouped:
-                c_grouped[m] = work.tile([P, O, PACK], BF16, name="c_grouped", align_bytes=64, bufs=3)
-            cols = slice(half * O // 2, (half + 1) * O // 2)
-            interleave(engine, c_grouped[m][:, cols, :], c_raw[m][:, :, cols])
+        def group_c(m, engine):
+            cg = work.tile([P, O, PACK], BF16, name="c_grouped", align_bytes=64, bufs=1)
+            interleave(engine, cg[:], c_raw[m][:])
+            c_grouped[m] = cg
 
         def quantize_c(m):
             c_quant[m] = quantize("c%d" % m, c_grouped[m][:].rearrange("p o t -> p (o t)"))
@@ -295,7 +290,7 @@ def tile_hermitechaosridgeexpansiondegreethree_w4_kernel(
             j, h = divmod(i, 2)
             first = gf == 0 and d == 0
             if first:
-                out_banks[i] = psum.tile([P, O], F32, name="acc", tag="acc%d" % h)
+                out_banks[i] = psum.tile([P, O], F32, name="acc", tag=("acc%d" if j % 2 == 0 else "turn%d") % h)
             k_codes, k_plane = k_quant[j * F_PASSES + gf, d, h]
             c_codes, c_plane = c_quant[d * F_PASSES + gf]
             nc.tensor.matmul_mx(
@@ -325,140 +320,97 @@ def tile_hermitechaosridgeexpansiondegreethree_w4_kernel(
             for h in range(2):
                 make_k3(s, h)
 
-        order_w(0)
-        order_w(1)
+        passes = [(gf, d) for gf in range(F_PASSES) for d in range(T)]
+
+        def read_passes(tiles, which):
+            for i in tiles:
+                for gf, d in which:
+                    readout(i, gf, d)
+
         widen_x(0)
         turn_x(0)
-        group_c(0, "scalar", 0)
-        empty_x(0)
         widen_x(1)
-        turn_x(1)
         turn_gains()
-        group_c(0, "scalar", 1)
-        empty_x(1)
+        order_w(0)
+        order_w(1)
+        scale_x(0)
+        turn_x(1)
         scale_gains()
+        widen_x(2)
+        widen_x(3)
+        turn_x(2)
         order_w_scales()
         quantize_x(0)
         project(0, 0)
-        widen_x(2)
+        scale_x(1)
         quantize_x(1)
         project(0, 1)
-        turn_x(2)
+        turn_x(3)
         project(1, 0)
         project(1, 1)
-        widen_x(3)
-        turn_x(3)
-        quantize_c(0)
-        group_c(1, "vector", 0)
-        scalar_part(0)
-        empty_x(2)
-        empty_x(3)
-        psum_part(0)
-        scalar_part(1)
-        group_c(1, "vector", 1)
+        scale_x(2)
+        group_c(0, "vector")
         quantize_x(2)
-        quantize_x(3)
-        project(2, 0)
-        project(2, 1)
-        make_k2(0, "vector")
-        quantize_k(0, 0)
-        quantize_k(0, 2)
         widen_x(4)
-        quantize_k(0, 1)
-        quantize_c(1)
-        group_c(2, "scalar", 0)
-        group_c(2, "scalar", 1)
-        psum_part(1)
-        project(3, 0)
-        project(3, 1)
-        scalar_part(2)
-        make_k2(1, "vector")
-        quantize_k(1, 0)
-        quantize_k(1, 2)
-        widen_x(5)
-        turn_x(4)
-        turn_x(5)
-        empty_x(4)
-        empty_x(5)
-        quantize_k(1, 1)
-        quantize_c(2)
-        psum_part(2)
-        scalar_part(3)
-        quantize_x(4)
-        quantize_x(5)
-        project(4, 0)
-        project(4, 1)
-        make_k2(2, "vector")
-        quantize_k(2, 0)
-        quantize_k(2, 2)
-        widen_x(6)
-        quantize_k(2, 1)
-        group_c(3, "scalar", 0)
-        group_c(3, "scalar", 1)
-        psum_part(3)
-        project(5, 0)
-        project(5, 1)
-        scalar_part(4)
-        make_k2(3, "vector")
-        quantize_k(3, 0)
-        quantize_k(3, 2)
-        widen_x(7)
-        turn_x(6)
-        turn_x(7)
-        empty_x(6)
-        empty_x(7)
-        quantize_k(3, 1)
-        quantize_c(3)
-        group_c(4, "scalar", 0)
-        group_c(4, "vector", 1)
-        psum_part(4)
-        scalar_part(5)
-        quantize_x(6)
-        quantize_x(7)
-        project(6, 0)
-        project(6, 1)
-        quantize_c(4)
-        make_k2(4, "vector")
-        group_c(5, "scalar", 0)
-        quantize_k(4, 0)
-        quantize_k(4, 2)
-        group_c(5, "vector", 1)
-        quantize_k(4, 1)
-        quantize_c(5)
-        readout_tile(0)
-        readout_tile(1)
-        psum_part(5)
-        project(7, 0)
-        project(7, 1)
-        make_k2(5, "scalar")
-        scalar_part(6)
-        finish(0)
-        readout_tile(2)
-        quantize_k(5, 0)
-        quantize_k(5, 2)
-        finish(1)
-        readout_tile(3)
-        quantize_k(5, 1)
-        psum_part(6)
-        make_k2(6, "scalar")
-        scalar_part(7)
-        finish(2)
-        readout_tile(4)
-        quantize_k(6, 0)
-        quantize_k(6, 2)
-        finish(3)
-        readout_tile(5)
-        quantize_k(6, 1)
+        squares_of(0)
+        make_cubic_factor(0)
+        make_k2_rows(0)
+        quantize_c(0)
+        for s in range(STEPS - 1):
+            if s + 1 < T * F_PASSES:
+                group_c(s + 1, "gpsimd")
+            if s + 3 < ROW_TILES:
+                scale_x(s + 3)
+            k2_engine = "vector" if s < 1 else "scalar" if s < 5 else "gpsimd"
+            if k2_engine == "gpsimd":
+                make_k2(s, k2_engine)
+            psum_part(s)
+            squares_of(s + 1)
+            if k2_engine == "scalar":
+                make_k2(s, k2_engine)
+            if s + 5 < ROW_TILES:
+                widen_x(s + 5)
+            make_cubic_factor(s + 1)
+            make_k2_rows(s + 1)
+            if s + 3 < ROW_TILES:
+                quantize_x(s + 3)
+            if s + 4 < ROW_TILES:
+                turn_x(s + 4)
+            if s == 4:
+                read_passes((0, 1), passes[:-1])
+            if s + 2 < STEPS:
+                project(s + 2, 0)
+                project(s + 2, 1)
+            if s == 5:
+                read_passes((3,), passes)
+            if s >= 5:
+                finish(2 * (s - 5))
+                finish(2 * (s - 5) + 1)
+            if k2_engine == "vector":
+                make_k2(s, k2_engine)
+            quantize_k(s, 0)
+            quantize_k(s, 2)
+            if s == 4:
+                quantize_c(5)
+            quantize_k(s, 1)
+            if s < 4:
+                quantize_c(s + 1)
+            if s == 4:
+                read_passes((0, 1), passes[-1:])
+                read_passes((2,), passes)
+            if s == 5:
+                read_passes((4, 5), passes)
+            if s == 6:
+                read_passes((6, 7), passes[:T])
         for h in range(2):
             make_k2(7, "scalar", slice(h * P, (h + 1) * P))
         for h in range(2):
-            finish(4 + h)
-            for d in range(T):
-                readout(6 + h, 0, d)
             make_k1(7, h)
             make_k3(7, h)
+            if h == 0:
+                finish(4)
             for d in range(T):
                 quantize_k_half(7, d, h)
                 readout(6 + h, 1, d)
-        finish(6)
-        finish(7)
+        for i in range(5, ROW_TILES):
+            finish(i)

@@ -41,6 +41,8 @@ def tile_hermitechaosridgeexpansiondegreethree_w4_kernel(
 
         ident = keep.tile([P, P], F32, name="ident")
         make_identity(nc, ident[:])
+        ident_bf = keep.tile([P, P], BF16, name="ident_bf")
+        nc.gpsimd.tensor_copy(out=ident_bf[:], in_=ident[:])
         ws_raw = keep.tile([P, D_PASSES * F // 4], I32, name="ws_raw")
         nc.vector.memset(ws_raw[:], 0)
         g_rows = keep.tile([P, PACK, P], F32, name="g_rows")
@@ -74,18 +76,21 @@ def tile_hermitechaosridgeexpansiondegreethree_w4_kernel(
             wr = keep.tile([P, F // 2], I32, name="w_raw%d" % gk)
             nc.sync.dma_start(out=wr[:], in_=w_words[gk].bitcast(I32))
             w_raw.append(wr)
+        load_x(2)
         for quad in range(4):
             nc.sync.dma_start(
                 out=ws_raw[32 * quad : 32 * quad + 4, :].rearrange("r (k n) -> r k n", k=D_PASSES),
                 in_=w_scales[:, 4 * quad : 4 * quad + 4, :].rearrange("k r n -> r k n").bitcast(I32),
             )
-        load_x(2)
         load_x(3)
+        load_x(4)
         load_c(0)
-        for i in range(4, ROW_TILES):
-            load_x(i)
-            load_c(i - 3)
-        load_c(5)
+        load_x(5)
+        load_x(6)
+        load_c(1)
+        load_x(7)
+        for m in range(2, T * F_PASSES):
+            load_c(m)
         bias = keep.tile([P, O], BF16, name="bias")
         nc.sync.dma_start(out=bias[:], in_=b.partition_broadcast(P))
 
@@ -104,7 +109,7 @@ def tile_hermitechaosridgeexpansiondegreethree_w4_kernel(
         def gain(name, d, factor):
             col = keep.tile([P, F_PASSES, PACK], F32, name=name)
             src = gains["bank"][:, :, d * F_PASSES : (d + 1) * F_PASSES].rearrange("p t h -> p h t")
-            nc.scalar.activation(out=col[:], in_=src, func=ACT.Copy, scale=factor)
+            nc.vector.tensor_scalar(out=col[:], in0=src, scalar1=factor, scalar2=None, op0=ALU.mult)
             gains[name] = col
 
         def scale_gains():
@@ -135,30 +140,43 @@ def tile_hermitechaosridgeexpansiondegreethree_w4_kernel(
         x_wide, x_turned, x_grouped, x_codes, x_planes = {}, {}, {}, {}, {}
 
         def widen_x(i):
-            xw = work.tile([P, D], BF16, name="x_wide", bufs=4)
+            xw = work.tile([P, D], BF16, name="x_wide", bufs=6)
             width = K_PASS if i == 0 else D
-            for start in range(0, D, width):
-                cols = slice(start, start + width)
-                nc.scalar.activation(out=xw[:, cols], in_=x_raw[i][:, cols].bitcast(FP8), func=ACT.Copy)
+            nc.scalar.activation(out=xw[:, :width], in_=x_raw[i][:, :width].bitcast(FP8), func=ACT.Copy)
+            if width < D:
+                nc.vector.tensor_copy(out=xw[:, width:], in_=x_raw[i][:, width:].bitcast(FP8))
             x_wide[i] = xw
 
         def turn_x(i):
             words = x_wide[i][:].bitcast(F32)
-            bank = psum.tile([P, D_PASSES, 2, P], F32, name="turn", tag="turn%d" % (i % 2))
+            bank = psum.tile([P, 2, D_PASSES, P], F32, name="turn", tag="turn%d" % (i % 2))
             for gk in range(D_PASSES):
                 for u in range(2):
-                    nc.tensor.transpose(bank[:, gk, u, :], words[:, 256 * gk + u : 256 * (gk + 1) : 2], ident[:])
+                    nc.tensor.transpose(bank[:, u, gk, :], words[:, 256 * gk + u : 256 * (gk + 1) : 2], ident[:])
             x_turned[i] = bank
 
+        stages = {}
+
+        def stage(s):
+            if s not in stages:
+                stages[s] = work.tile([P, 4, CHUNK * PACK], BF16, name="stage", align_bytes=64)
+            return stages[s]
+
         def scale_x(i):
-            xg = work.tile([P, D_PASSES, P, 2, 2], BF16, name="x_grouped", align_bytes=64)
-            for gk in range(D_PASSES):
-                nc.vector.tensor_tensor(
-                    out=xg[:, gk],
-                    in0=x_turned[i][:, gk].bitcast(BF16).rearrange("p u (r e) -> p r u e", e=2),
-                    in1=xs_col[:, gk : gk + 1, :].rearrange("p o (u e) -> p o u e", e=2).to_broadcast([P, P, 2, 2]),
-                    op=ALU.mult,
-                )
+            if i == 0:
+                xg = keep.tile([P, D], BF16, name="x0_grouped", align_bytes=64)[:]
+            elif i == 1:
+                xg = work.tile([P, D], BF16, name="c_grouped", align_bytes=64, bufs=1)[:]
+            elif i < 4:
+                if i == 2:
+                    stages["x23"] = keep.tile([P, 2, D], BF16, name="x23_grouped", align_bytes=64)
+                xg = stages["x23"][:, i - 2, :]
+            else:
+                xg = stage(i - 4)[:, 3, :]
+            dst = xg.rearrange("p (k r u e) -> p k r u e", k=D_PASSES, u=2, e=2)
+            turned = x_turned[i][:].bitcast(BF16).rearrange("p u k (r e) -> p k r u e", e=2)
+            scales = xs_col[:].rearrange("p k (o u e) -> p k o u e", o=1, e=2).to_broadcast([P, D_PASSES, P, 2, 2])
+            nc.vector.tensor_tensor(out=dst, in0=turned, in1=scales, op=ALU.mult)
             x_grouped[i] = xg
 
         def quantize(name, src):
@@ -169,7 +187,13 @@ def tile_hermitechaosridgeexpansiondegreethree_w4_kernel(
             return codes, plane
 
         def quantize_x(i):
-            x_codes[i], x_planes[i] = quantize("x%d" % i, x_grouped[i][:].rearrange("p k r u e -> p (k r u e)"))
+            x_codes[i], x_planes[i] = quantize("x%d" % i, x_grouped[i])
+
+        def quantize_x23():
+            codes, plane = quantize("x23", stages["x23"][:].rearrange("p a w -> p (a w)"))
+            for i in (2, 3):
+                cols = slice((i - 2) * CHUNK, (i - 1) * CHUNK)
+                x_codes[i], x_planes[i] = codes[:, cols], plane[:, cols]
 
         u_banks = {}
 
@@ -223,13 +247,27 @@ def tile_hermitechaosridgeexpansiondegreethree_w4_kernel(
 
         k_grouped, k_quant = {}, {}
 
+        slot_of = {0: 0, 2: 1, 1: 2}
+
         def grouped(s, d):
             if (s, d) not in k_grouped:
                 if d == 1 and 4 <= s <= 6:
-                    k_grouped[s, d] = work.tile([P, CHUNK, PACK], BF16, name="k2_late", align_bytes=64, bufs=1)
+                    kg = work.tile([P, CHUNK * PACK], BF16, name="k2_late", align_bytes=64, bufs=1)[:]
                 else:
-                    k_grouped[s, d] = work.tile([P, CHUNK, PACK], BF16, name="k%d_grouped" % (d + 1), align_bytes=64)
+                    kg = stage(s)[:, slot_of[d], :]
+                k_grouped[s, d] = kg.rearrange("p (n t) -> p n t", t=PACK)
             return k_grouped[s, d]
+
+        def quantize_stage(s, parts):
+            codes, plane = quantize("stage%d" % s, stage(s)[:, :parts, :].rearrange("p a w -> p (a w)"))
+            for d in range(T):
+                if slot_of[d] < parts:
+                    for h in range(2):
+                        cols = slice(slot_of[d] * CHUNK + h * P, slot_of[d] * CHUNK + (h + 1) * P)
+                        k_quant[s, d, h] = codes[:, cols], plane[:, cols]
+            if parts == 4:
+                cols = slice(3 * CHUNK, 4 * CHUNK)
+                x_codes[s + 4], x_planes[s + 4] = codes[:, cols], plane[:, cols]
 
         def make_k1(s, h):
             gf = s % F_PASSES
@@ -264,22 +302,35 @@ def tile_hermitechaosridgeexpansiondegreethree_w4_kernel(
         def make_k2(s, engine, cols=slice(0, CHUNK)):
             interleave(engine, grouped(s, 1)[:, cols, :], k2_rows[s][:, :, cols])
 
+        k2_banks = {}
+
+        def weave_k2(s):
+            bank = psum.tile([P, CHUNK, PACK], BF16, name="weave", tag="acc%d" % (s % 2))
+            for h in range(2):
+                cols = slice(h * P, (h + 1) * P)
+                nc.tensor.matmul(
+                    out=bank[:, cols, :].rearrange("p (n i) t -> p n t i", i=8),
+                    lhsT=ident_bf[:],
+                    rhs=k2_rows[s][:, :, cols].rearrange("p t (n i) -> p n t i", i=8),
+                    start=True,
+                    stop=True,
+                )
+            k2_banks[s] = bank
+
+        def empty_k2(s):
+            nc.scalar.copy(out=grouped(s, 1), in_=k2_banks[s][:])
+
         def quantize_k(s, d):
-            codes, plane = quantize("k%d_%d" % (d + 1, s), k_grouped[s, d][:].rearrange("p n t -> p (n t)"))
+            codes, plane = quantize("k%d_%d" % (d + 1, s), k_grouped[s, d].rearrange("p n t -> p (n t)"))
             for h in range(2):
                 k_quant[s, d, h] = codes[:, h * P : (h + 1) * P], plane[:, h * P : (h + 1) * P]
 
-        def quantize_k_half(s, d, h):
-            src = k_grouped[s, d][:, h * P : (h + 1) * P, :].rearrange("p n t -> p (n t)")
-            codes, plane = quantize("k%d_%d_%d" % (d + 1, s, h), src)
-            k_quant[s, d, h] = codes[:], plane[:]
-
         c_grouped, c_quant = {}, {}
 
-        def group_c(m, engine):
-            cg = work.tile([P, O, PACK], BF16, name="c_grouped", align_bytes=64, bufs=1)
-            interleave(engine, cg[:], c_raw[m][:])
-            c_grouped[m] = cg
+        def group_c(m, engine, cols=slice(0, O)):
+            if m not in c_grouped:
+                c_grouped[m] = work.tile([P, O, PACK], BF16, name="c_grouped", align_bytes=64, bufs=1)
+            interleave(engine, c_grouped[m][:, cols, :], c_raw[m][:, :, cols])
 
         def quantize_c(m):
             c_quant[m] = quantize("c%d" % m, c_grouped[m][:].rearrange("p o t -> p (o t)"))
@@ -309,18 +360,13 @@ def tile_hermitechaosridgeexpansiondegreethree_w4_kernel(
                     readout(i, gf, d)
 
         def finish(i):
-            res = work.tile([P, O], F32, name="result", bufs=3)
+            res = work.tile([P, O], F32, name="result", bufs=4)
             nc.vector.tensor_tensor(out=res[:], in0=out_banks[i][:], in1=bias[:], op=ALU.add)
             nc.sync.dma_start(out=out[i * P : (i + 1) * P, :], in_=res[:])
 
+        WOVEN = 3
 
-        def psum_part(s):
-            for h in range(2):
-                make_k1(s, h)
-            for h in range(2):
-                make_k3(s, h)
-
-        passes = [(gf, d) for gf in range(F_PASSES) for d in range(T)]
+        passes = [(gf, d) for d in range(T) for gf in range(F_PASSES)]
 
         def read_passes(tiles, which):
             for i in tiles:
@@ -335,7 +381,6 @@ def tile_hermitechaosridgeexpansiondegreethree_w4_kernel(
         order_w(1)
         scale_x(0)
         turn_x(1)
-        scale_gains()
         widen_x(2)
         widen_x(3)
         turn_x(2)
@@ -348,69 +393,84 @@ def tile_hermitechaosridgeexpansiondegreethree_w4_kernel(
         turn_x(3)
         project(1, 0)
         project(1, 1)
+        group_c(0, "gpsimd")
         scale_x(2)
-        group_c(0, "vector")
-        quantize_x(2)
+        scale_gains()
         widen_x(4)
-        squares_of(0)
+        turn_x(4)
+        widen_x(5)
+        square(0, 0)
+        square(0, 1)
         make_cubic_factor(0)
         make_k2_rows(0)
+        weave_k2(0)
+        squares_of(1)
+        make_k1(0, 0)
+        scale_x(3)
+        make_k1(0, 1)
+        quantize_x23()
         quantize_c(0)
         for s in range(STEPS - 1):
-            if s + 1 < T * F_PASSES:
+            if s < 4:
                 group_c(s + 1, "gpsimd")
-            if s + 3 < ROW_TILES:
-                scale_x(s + 3)
-            k2_engine = "vector" if s < 1 else "scalar" if s < 5 else "gpsimd"
-            if k2_engine == "gpsimd":
-                make_k2(s, k2_engine)
-            psum_part(s)
-            squares_of(s + 1)
-            if k2_engine == "scalar":
-                make_k2(s, k2_engine)
-            if s + 5 < ROW_TILES:
-                widen_x(s + 5)
-            make_cubic_factor(s + 1)
-            make_k2_rows(s + 1)
-            if s + 3 < ROW_TILES:
-                quantize_x(s + 3)
+            elif s == 4:
+                group_c(5, "gpsimd", slice(0, 320))
+            else:
+                make_k2(s, "gpsimd")
             if s + 4 < ROW_TILES:
-                turn_x(s + 4)
-            if s == 4:
-                read_passes((0, 1), passes[:-1])
+                scale_x(s + 4)
+            if s + 5 < ROW_TILES:
+                turn_x(s + 5)
+            make_k3(s, 0)
+            make_k3(s, 1)
             if s + 2 < STEPS:
                 project(s + 2, 0)
                 project(s + 2, 1)
-            if s == 5:
-                read_passes((3,), passes)
+            if s == 3:
+                read_passes((0, 1), passes[:4])
+            if s == 4:
+                read_passes((0, 1), passes[4:5])
+                read_passes((2, 3), passes[:5])
+            if s in (3, 4):
+                make_k2(s, "scalar")
+            if s == 4:
+                group_c(5, "scalar", slice(320, O))
+            if s + 6 < ROW_TILES:
+                widen_x(s + 6)
+            if s < 2:
+                empty_k2(s)
+            make_cubic_factor(s + 1)
+            if 2 <= s < WOVEN:
+                empty_k2(s)
+            make_k2_rows(s + 1)
+            if s + 1 < WOVEN:
+                weave_k2(s + 1)
+            make_k1(s + 1, 0)
+            make_k1(s + 1, 1)
+            if s + 2 < STEPS:
+                squares_of(s + 2)
             if s >= 5:
                 finish(2 * (s - 5))
                 finish(2 * (s - 5) + 1)
-            if k2_engine == "vector":
-                make_k2(s, k2_engine)
-            quantize_k(s, 0)
-            quantize_k(s, 2)
-            if s == 4:
-                quantize_c(5)
-            quantize_k(s, 1)
-            if s < 4:
+            quantize_stage(s, 4 if s < 4 else 2)
+            if s < 5:
                 quantize_c(s + 1)
+            if s == 6:
+                quantize_k(7, 0)
+            if s >= 4:
+                quantize_k(s, 1)
             if s == 4:
-                read_passes((0, 1), passes[-1:])
-                read_passes((2,), passes)
+                read_passes((0, 1, 2, 3), passes[5:])
             if s == 5:
                 read_passes((4, 5), passes)
             if s == 6:
-                read_passes((6, 7), passes[:T])
-        for h in range(2):
-            make_k2(7, "scalar", slice(h * P, (h + 1) * P))
-        for h in range(2):
-            make_k1(7, h)
-            make_k3(7, h)
-            if h == 0:
-                finish(4)
-            for d in range(T):
-                quantize_k_half(7, d, h)
-                readout(6 + h, 1, d)
-        for i in range(5, ROW_TILES):
+                for one in [(0, 0), (0, 2), (1, 0), (0, 1)]:
+                    read_passes((6, 7), [one])
+        make_k2(7, "scalar")
+        make_k3(7, 0)
+        make_k3(7, 1)
+        quantize_k(7, 1)
+        quantize_k(7, 2)
+        read_passes((6, 7), [(1, 1), (1, 2)])
+        for i in range(4, ROW_TILES):
             finish(i)

@@ -159,7 +159,7 @@ def tile_hermitechaosridgeexpansiondegreethree_w4_kernel(
 
         def stage(s):
             if s not in stages:
-                stages[s] = work.tile([P, 4, CHUNK * PACK], BF16, name="stage", align_bytes=64)
+                stages[s] = work.tile([P, 4, CHUNK * PACK], BF16, name="stage", align_bytes=64, bufs=3)
             return stages[s]
 
         def scale_x(i):
@@ -218,7 +218,7 @@ def tile_hermitechaosridgeexpansiondegreethree_w4_kernel(
         squares, cubic_factor, k2_rows = {}, {}, {}
 
         def square(s, h):
-            if h == 0:
+            if s not in squares:
                 squares[s] = work.tile([P, PACK, CHUNK], F32, name="square")
             nc.scalar.activation(out=squares[s][:, :, h * P : (h + 1) * P], in_=u_banks[s, h][:], func=ACT.Square)
 
@@ -234,8 +234,8 @@ def tile_hermitechaosridgeexpansiondegreethree_w4_kernel(
                 )
 
         def squares_of(s):
-            square(s, 0)
             square(s, 1)
+            square(s, 0)
 
         def make_cubic_factor(s):
             cubic_factor[s] = work.tile([P, PACK, CHUNK], F32, name="cubic_factor")
@@ -305,7 +305,7 @@ def tile_hermitechaosridgeexpansiondegreethree_w4_kernel(
         k2_banks = {}
 
         def weave_k2(s):
-            bank = psum.tile([P, CHUNK, PACK], BF16, name="weave", tag="acc%d" % (s % 2))
+            bank = psum.tile([P, CHUNK, PACK], BF16, name="weave", tag="acc%d" % (s % 2) if s < 4 else "turn0")
             for h in range(2):
                 cols = slice(h * P, (h + 1) * P)
                 nc.tensor.matmul(
@@ -339,7 +339,7 @@ def tile_hermitechaosridgeexpansiondegreethree_w4_kernel(
 
         def readout(i, gf, d):
             j, h = divmod(i, 2)
-            first = gf == 0 and d == 0
+            first = i not in out_banks
             if first:
                 out_banks[i] = psum.tile([P, O], F32, name="acc", tag=("acc%d" if j % 2 == 0 else "turn%d") % h)
             k_codes, k_plane = k_quant[j * F_PASSES + gf, d, h]
@@ -360,11 +360,11 @@ def tile_hermitechaosridgeexpansiondegreethree_w4_kernel(
                     readout(i, gf, d)
 
         def finish(i):
-            res = work.tile([P, O], F32, name="result", bufs=4)
+            res = keep.tile([P, O], F32, name="result%d" % i)
             nc.vector.tensor_tensor(out=res[:], in0=out_banks[i][:], in1=bias[:], op=ALU.add)
             nc.sync.dma_start(out=out[i * P : (i + 1) * P, :], in_=res[:])
 
-        WOVEN = 3
+        WOVEN = 5
 
         passes = [(gf, d) for d in range(T) for gf in range(F_PASSES)]
 
@@ -408,8 +408,8 @@ def tile_hermitechaosridgeexpansiondegreethree_w4_kernel(
         make_k1(0, 0)
         scale_x(3)
         make_k1(0, 1)
-        quantize_x23()
         quantize_c(0)
+        quantize_x23()
         for s in range(STEPS - 1):
             if s < 4:
                 group_c(s + 1, "gpsimd")
@@ -417,8 +417,6 @@ def tile_hermitechaosridgeexpansiondegreethree_w4_kernel(
                 group_c(5, "gpsimd", slice(0, 320))
             else:
                 make_k2(s, "gpsimd")
-            if s + 4 < ROW_TILES:
-                scale_x(s + 4)
             if s + 5 < ROW_TILES:
                 turn_x(s + 5)
             make_k3(s, 0)
@@ -430,9 +428,8 @@ def tile_hermitechaosridgeexpansiondegreethree_w4_kernel(
                 read_passes((0, 1), passes[:4])
             if s == 4:
                 read_passes((0, 1), passes[4:5])
-                read_passes((2, 3), passes[:5])
-            if s in (3, 4):
-                make_k2(s, "scalar")
+            if s == 5:
+                read_passes((3,), passes)
             if s == 4:
                 group_c(5, "scalar", slice(320, O))
             if s + 6 < ROW_TILES:
@@ -445,26 +442,29 @@ def tile_hermitechaosridgeexpansiondegreethree_w4_kernel(
             make_k2_rows(s + 1)
             if s + 1 < WOVEN:
                 weave_k2(s + 1)
-            make_k1(s + 1, 0)
             make_k1(s + 1, 1)
+            if s + 4 < ROW_TILES:
+                scale_x(s + 4)
+            make_k1(s + 1, 0)
             if s + 2 < STEPS:
                 squares_of(s + 2)
             if s >= 5:
-                finish(2 * (s - 5))
                 finish(2 * (s - 5) + 1)
-            quantize_stage(s, 4 if s < 4 else 2)
+                finish(2 * (s - 5))
             if s < 5:
                 quantize_c(s + 1)
-            if s == 6:
-                quantize_k(7, 0)
             if s >= 4:
                 quantize_k(s, 1)
+            quantize_stage(s, 4 if s < 4 else 2)
+            if s == 6:
+                quantize_k(7, 0)
             if s == 4:
-                read_passes((0, 1, 2, 3), passes[5:])
+                read_passes((0, 1), passes[5:])
+                read_passes((2,), passes)
             if s == 5:
                 read_passes((4, 5), passes)
             if s == 6:
-                for one in [(0, 0), (0, 2), (1, 0), (0, 1)]:
+                for one in [(0, 1), (0, 0), (0, 2), (1, 0)]:
                     read_passes((6, 7), [one])
         make_k2(7, "scalar")
         make_k3(7, 0)

@@ -19,14 +19,31 @@ ALU = mybir.AluOpType
 ACT = mybir.ActivationFunctionType
 
 P = 128
-PACK = 4
-K_PASS = P * PACK
-D_PASSES = D // K_PASS
-F_PASSES = F // K_PASS
-ROW_TILES = N // P
-CHUNK = 2 * P
-STEPS = (N // CHUNK) * F_PASSES
+SLOTS = 4
+PASS = P * SLOTS
+K_PASSES = D // PASS
+F_PASSES = F // PASS
 RUN = 8
+BLOCKS = PASS // 32
+TILES = N // P
+STEP_TOKENS = 2 * P
+STEPS = (N // STEP_TOKENS) * F_PASSES
+LAST = STEPS - 1
+C_PARTS = T * F_PASSES
+
+K1, K2, K3 = 0, 1, 2
+QUARTER = {K1: 0, K3: 1, K2: 2}
+X_QUARTER = 3
+HEAD_TILES = 4
+X_STEPS = TILES - HEAD_TILES
+
+TENSOR_K2_STEPS = C_PARTS - 1
+LAST_C_SPLIT = 320
+
+TURN_BANKS = ("side0", "side1")
+WEAVE_BANK = "side2"
+SPARE_BANK = "side3"
+SUM_BANKS = (SPARE_BANK, TURN_BANKS[0], TURN_BANKS[1], WEAVE_BANK)
 
 
 def tile_hermitechaosridgeexpansiondegreethree_w4_kernel(
@@ -39,438 +56,425 @@ def tile_hermitechaosridgeexpansiondegreethree_w4_kernel(
         psum = ctx.enter_context(tc.psum_pool(name="psum", bufs=1))
         ctx.enter_context(tc.manual_schedule())
 
+        g_raw = keep.tile([C_PARTS, PASS], BF16, name="g_raw")
+        nc.gpsimd.dma_start(out=g_raw[:], in_=g.rearrange("d (e f) -> (d e) f", e=F_PASSES))
         ident = keep.tile([P, P], F32, name="ident")
         make_identity(nc, ident[:])
         ident_bf = keep.tile([P, P], BF16, name="ident_bf")
         nc.gpsimd.tensor_copy(out=ident_bf[:], in_=ident[:])
-        ws_raw = keep.tile([P, D_PASSES * F // 4], I32, name="ws_raw")
-        nc.vector.memset(ws_raw[:], 0)
-        g_rows = keep.tile([P, PACK, P], F32, name="g_rows")
+        w_scale_raw = keep.tile([P, K_PASSES * F // 4], I32, name="w_scale_raw")
+        nc.vector.memset(w_scale_raw[:], 0)
+        g_rows = keep.tile([P, SLOTS, P], F32, name="g_rows")
         nc.vector.memset(g_rows[:], 0.0)
 
-        x_raw = []
+        x_raw, c_rows = {}, {}
 
         def load_x(i):
-            xr = keep.tile([P, D], U8, name="x_raw%d" % i)
-            nc.sync.dma_start(out=xr[:], in_=x_bytes[i * P : (i + 1) * P, :])
-            x_raw.append(xr)
-
-        c_raw = {}
+            x_raw[i] = keep.tile([P, D], U8, name="x_raw%d" % i)
+            nc.sync.dma_start(out=x_raw[i][:], in_=x_bytes[i * P : (i + 1) * P, :])
 
         def load_c(m):
-            d, gf = divmod(m, F_PASSES)
-            cr = keep.tile([P, PACK, O], BF16, name="c_raw%d" % m)
-            rows = c[d, gf * K_PASS : (gf + 1) * K_PASS, :].rearrange("(q t r) o -> t q r o", t=PACK, r=RUN)
-            for t in range(PACK):
-                nc.sync.dma_start(out=cr[:, t, :], in_=rows[t])
-            c_raw[m] = cr
+            d, e = divmod(m, F_PASSES)
+            c_rows[m] = keep.tile([P, SLOTS, O], BF16, name="c_rows%d" % m)
+            by_slot = c[d, e * PASS : (e + 1) * PASS, :].rearrange("(q t r) o -> t q r o", t=SLOTS, r=RUN)
+            for t in range(SLOTS):
+                nc.sync.dma_start(out=c_rows[m][:, t, :], in_=by_slot[t])
 
         load_x(0)
-        xs_col = keep.tile([P, D_PASSES, PACK], F32, name="xs_col")
-        nc.sync.dma_start(out=xs_col[:], in_=x_scale.rearrange("o (k p j) -> p (o k) j", p=P, j=PACK))
+        x_scales = keep.tile([P, K_PASSES, SLOTS], F32, name="x_scales")
+        nc.sync.dma_start(out=x_scales[:], in_=x_scale.rearrange("o (a p t) -> p (o a) t", p=P, t=SLOTS))
         load_x(1)
-        g_raw = keep.tile([T * F_PASSES, K_PASS], BF16, name="g_raw")
-        nc.sync.dma_start(out=g_raw[:], in_=g.rearrange("d (h f) -> (d h) f", h=F_PASSES))
-        w_raw = []
-        for gk in range(D_PASSES):
-            wr = keep.tile([P, F // 2], I32, name="w_raw%d" % gk)
-            nc.sync.dma_start(out=wr[:], in_=w_words[gk].bitcast(I32))
-            w_raw.append(wr)
-        load_x(2)
-        for quad in range(4):
+        w_raw = keep.tile([P, K_PASSES, F // 2], I32, name="w_raw")
+        nc.sync.dma_start(out=w_raw[:], in_=w_words.rearrange("a p n -> p a n").bitcast(I32))
+        for j in range(4):
             nc.sync.dma_start(
-                out=ws_raw[32 * quad : 32 * quad + 4, :].rearrange("r (k n) -> r k n", k=D_PASSES),
-                in_=w_scales[:, 4 * quad : 4 * quad + 4, :].rearrange("k r n -> r k n").bitcast(I32),
+                out=w_scale_raw[32 * j : 32 * j + 4, :].rearrange("r (a n) -> r a n", a=K_PASSES),
+                in_=w_scales[:, 4 * j : 4 * j + 4, :].rearrange("a r n -> r a n").bitcast(I32),
             )
-        load_x(3)
-        load_x(4)
+        for i in (2, 3, 4):
+            load_x(i)
         load_c(0)
         load_x(5)
         load_x(6)
         load_c(1)
         load_x(7)
-        for m in range(2, T * F_PASSES):
+        for m in range(2, C_PARTS):
             load_c(m)
         bias = keep.tile([P, O], BF16, name="bias")
         nc.sync.dma_start(out=bias[:], in_=b.partition_broadcast(P))
 
-        gains = {}
-
         def turn_gains():
             nc.vector.tensor_copy(
-                out=g_rows[0 : T * F_PASSES].rearrange("m t (q r) -> m t q r", r=RUN),
-                in_=g_raw[:].rearrange("m (q t r) -> m t q r", t=PACK, r=RUN),
+                out=g_rows[0:C_PARTS].rearrange("m t (q r) -> m t q r", r=RUN),
+                in_=g_raw[:].rearrange("m (q t r) -> m t q r", t=SLOTS, r=RUN),
             )
-            g_bank = psum.tile([P, PACK, P], F32, name="g_bank", tag="acc0")
-            for t in range(PACK):
-                nc.tensor.transpose(g_bank[:, t, :], g_rows[:, t, :], ident[:])
-            gains["bank"] = g_bank
+            bank = psum.tile([P, SLOTS, P], F32, name="g_bank", tag=WEAVE_BANK)
+            for t in range(SLOTS):
+                nc.tensor.transpose(bank[:, t, :], g_rows[:, t, :], ident[:])
+            return bank
 
-        def gain(name, d, factor):
-            col = keep.tile([P, F_PASSES, PACK], F32, name=name)
-            src = gains["bank"][:, :, d * F_PASSES : (d + 1) * F_PASSES].rearrange("p t h -> p h t")
-            nc.vector.tensor_scalar(out=col[:], in0=src, scalar1=factor, scalar2=None, op0=ALU.mult)
-            gains[name] = col
+        def gain(name, bank, d, factor):
+            scaled = keep.tile([P, F_PASSES, SLOTS], F32, name=name)
+            src = bank[:, :, d * F_PASSES : (d + 1) * F_PASSES].rearrange("p t e -> p e t")
+            nc.vector.tensor_scalar(out=scaled[:], in0=src, scalar1=factor, scalar2=None, op0=ALU.mult)
+            return scaled
 
-        def scale_gains():
-            gain("g1", 0, 1.0)
-            gain("g3_mul", 2, 1.0 / math.sqrt(6.0))
-            gain("g3_add", 2, -3.0 / math.sqrt(6.0))
-            gain("g2_mul", 1, 1.0 / math.sqrt(2.0))
-            gain("g2_add", 1, -1.0 / math.sqrt(2.0))
-
-        w_codes, w_planes = [], []
-
-        def order_w(gk):
-            wc = keep.tile([P, 2 * F], U8, name="w_codes%d" % gk, align_bytes=64)
+        def order_w_codes(a):
+            codes = keep.tile([P, 2 * F], U8, name="w_codes%d" % a, align_bytes=64)
             nc.vector.tensor_copy(
-                out=wc[:].bitcast(I32).rearrange("p (h t q w) -> p h t q w", h=F_PASSES, t=PACK, w=4),
-                in_=w_raw[gk][:].rearrange("p (h q t w) -> p h t q w", h=F_PASSES, t=PACK, w=4),
+                out=codes[:].bitcast(I32).rearrange("p (e t q w) -> p e t q w", e=F_PASSES, t=SLOTS, w=4),
+                in_=w_raw[:, a, :].rearrange("p (e q t w) -> p e t q w", e=F_PASSES, t=SLOTS, w=4),
             )
-            w_codes.append(wc)
+            return codes
 
         def order_w_scales():
-            wp = keep.tile([P, D_PASSES * F], U8, name="w_plane", align_bytes=64)
+            scales = keep.tile([P, K_PASSES * F], U8, name="w_scale", align_bytes=64)
             nc.vector.tensor_copy(
-                out=wp[:].bitcast(I32).rearrange("p (h t q w) -> p h t q w", t=PACK, q=16, w=2),
-                in_=ws_raw[:].rearrange("p (h q t w) -> p h t q w", t=PACK, q=16, w=2),
+                out=scales[:].bitcast(I32).rearrange("p (ae t q w) -> p ae t q w", t=SLOTS, q=BLOCKS, w=2),
+                in_=w_scale_raw[:].rearrange("p (ae q t w) -> p ae t q w", t=SLOTS, q=BLOCKS, w=2),
             )
-            w_planes.append(wp)
+            return scales
 
-        x_wide, x_turned, x_grouped, x_codes, x_planes = {}, {}, {}, {}, {}
+        def quantize(name, woven):
+            width = woven.shape[1] // SLOTS
+            codes = keep.tile([P, width], U32, name=name + "_codes", align_bytes=64)
+            scales = keep.tile([P, width], U8, name=name + "_scales", align_bytes=64)
+            nc.vector.quantize_mx(out=codes[:].bitcast(FP8X4), scales=scales[:], in_=woven)
+            return codes, scales
+
+        step_tiles = {}
+
+        def step_tile(s):
+            if s not in step_tiles:
+                step_tiles[s] = work.tile([P, 4, STEP_TOKENS * SLOTS], BF16, name="step_tile", align_bytes=64, bufs=3)
+            return step_tiles[s]
+
+        def gpsimd_tile(shape, tag):
+            return work.tile(shape, BF16, name=tag, align_bytes=64, bufs=1)
+
+        x_wide, x_turned, x_woven, x_mx = {}, {}, {}, {}
 
         def widen_x(i):
-            xw = work.tile([P, D], BF16, name="x_wide", bufs=6)
-            width = K_PASS if i == 0 else D
-            nc.scalar.activation(out=xw[:, :width], in_=x_raw[i][:, :width].bitcast(FP8), func=ACT.Copy)
-            if width < D:
-                nc.vector.tensor_copy(out=xw[:, width:], in_=x_raw[i][:, width:].bitcast(FP8))
-            x_wide[i] = xw
+            x_wide[i] = work.tile([P, D], BF16, name="x_wide", bufs=6)
+            start = PASS if i == 0 else 0
+            if start:
+                nc.vector.tensor_copy(out=x_wide[i][:, :start], in_=x_raw[i][:, :start].bitcast(FP8))
+            nc.scalar.activation(out=x_wide[i][:, start:], in_=x_raw[i][:, start:].bitcast(FP8), func=ACT.Copy)
+
+        def turn_pass(i, a, dst):
+            words = x_wide[i][:].bitcast(F32)
+            for j in range(2):
+                nc.tensor.transpose(dst[:, j, :], words[:, 256 * a + j : 256 * (a + 1) : 2], ident[:])
 
         def turn_x(i):
-            words = x_wide[i][:].bitcast(F32)
-            bank = psum.tile([P, 2, D_PASSES, P], F32, name="turn", tag="turn%d" % (i % 2))
-            for gk in range(D_PASSES):
-                for u in range(2):
-                    nc.tensor.transpose(bank[:, u, gk, :], words[:, 256 * gk + u : 256 * (gk + 1) : 2], ident[:])
-            x_turned[i] = bank
+            x_turned[i] = psum.tile([P, 2, K_PASSES, P], F32, name="x_turned", tag=TURN_BANKS[i % 2])
+            for a in range(K_PASSES):
+                turn_pass(i, a, x_turned[i][:, :, a, :])
 
-        stages = {}
+        def scale_x(i, woven):
+            nc.vector.tensor_tensor(
+                out=woven.rearrange("p (a n j h) -> p a n j h", a=K_PASSES, j=2, h=2),
+                in0=x_turned[i][:].bitcast(BF16).rearrange("p j a (n h) -> p a n j h", h=2),
+                in1=x_scales[:].rearrange("p a (o j h) -> p a o j h", o=1, h=2).to_broadcast([P, K_PASSES, P, 2, 2]),
+                op=ALU.mult,
+            )
+            x_woven[i] = woven
 
-        def stage(s):
-            if s not in stages:
-                stages[s] = work.tile([P, 4, CHUNK * PACK], BF16, name="stage", align_bytes=64, bufs=3)
-            return stages[s]
+        def turn_first_tile():
+            for a, tag in enumerate((TURN_BANKS[0], SPARE_BANK)):
+                x_turned[0, a] = psum.tile([P, 2, P], F32, name="x_turned", tag=tag)
+                turn_pass(0, a, x_turned[0, a][:])
 
-        def scale_x(i):
-            if i == 0:
-                xg = keep.tile([P, D], BF16, name="x0_grouped", align_bytes=64)[:]
-            elif i == 1:
-                xg = work.tile([P, D], BF16, name="c_grouped", align_bytes=64, bufs=1)[:]
-            elif i < 4:
-                if i == 2:
-                    stages["x23"] = keep.tile([P, 2, D], BF16, name="x23_grouped", align_bytes=64)
-                xg = stages["x23"][:, i - 2, :]
-            else:
-                xg = stage(i - 4)[:, 3, :]
-            dst = xg.rearrange("p (k r u e) -> p k r u e", k=D_PASSES, u=2, e=2)
-            turned = x_turned[i][:].bitcast(BF16).rearrange("p u k (r e) -> p k r u e", e=2)
-            scales = xs_col[:].rearrange("p k (o u e) -> p k o u e", o=1, e=2).to_broadcast([P, D_PASSES, P, 2, 2])
-            nc.vector.tensor_tensor(out=dst, in0=turned, in1=scales, op=ALU.mult)
-            x_grouped[i] = xg
-
-        def quantize(name, src):
-            width = src.shape[1] // PACK
-            codes = keep.tile([P, width], U32, name=name + "_codes", align_bytes=64)
-            plane = keep.tile([P, width], U8, name=name + "_plane", align_bytes=64)
-            nc.vector.quantize_mx(out=codes[:].bitcast(FP8X4), scales=plane[:], in_=src)
-            return codes, plane
-
-        def quantize_x(i):
-            x_codes[i], x_planes[i] = quantize("x%d" % i, x_grouped[i])
-
-        def quantize_x23():
-            codes, plane = quantize("x23", stages["x23"][:].rearrange("p a w -> p (a w)"))
-            for i in (2, 3):
-                cols = slice((i - 2) * CHUNK, (i - 1) * CHUNK)
-                x_codes[i], x_planes[i] = codes[:, cols], plane[:, cols]
-
-        u_banks = {}
-
-        def project(s, h):
-            j, gf = divmod(s, F_PASSES)
-            i = 2 * j + h
-            bank = psum.tile([P, PACK, P], F32, name="u", tag="u%d" % ((2 * s + h) % 4))
-            for t in range(PACK):
-                col = (gf * PACK + t) * P
-                for gk in range(D_PASSES):
-                    nc.tensor.matmul_mx(
-                        out=bank[:, t, :],
-                        lhsT=w_codes[gk][:, 2 * col : 2 * (col + P)].bitcast(FP4X4),
-                        lhsT_scale=w_planes[0][:, gk * F + col : gk * F + col + P],
-                        rhs=x_codes[i][:, gk * P : (gk + 1) * P].bitcast(FP8X4),
-                        rhs_scale=x_planes[i][:, gk * P : (gk + 1) * P],
-                        start=(gk == 0),
-                        stop=(gk == D_PASSES - 1),
-                    )
-            u_banks[s, h] = bank
-
-        squares, cubic_factor, k2_rows = {}, {}, {}
-
-        def square(s, h):
-            if s not in squares:
-                squares[s] = work.tile([P, PACK, CHUNK], F32, name="square")
-            nc.scalar.activation(out=squares[s][:, :, h * P : (h + 1) * P], in_=u_banks[s, h][:], func=ACT.Square)
-
-        def affine(s, dst, mul, add):
-            gf = s % F_PASSES
-            for t in range(PACK):
-                nc.scalar.activation(
-                    out=dst[:, t, :],
-                    in_=squares[s][:, t, :],
-                    func=ACT.Identity,
-                    scale=mul[:, gf, t : t + 1],
-                    bias=add[:, gf, t : t + 1],
+        def scale_first_tile():
+            x_woven[0] = keep.tile([P, D], BF16, name="x0_woven", align_bytes=64)[:]
+            for a in range(K_PASSES):
+                nc.vector.tensor_tensor(
+                    out=x_woven[0][:, a * PASS : (a + 1) * PASS].rearrange("p (n j h) -> p n j h", j=2, h=2),
+                    in0=x_turned[0, a][:].bitcast(BF16).rearrange("p j (n h) -> p n j h", h=2),
+                    in1=x_scales[:, a : a + 1, :].rearrange("p o (j h) -> p o j h", h=2).to_broadcast([P, P, 2, 2]),
+                    op=ALU.mult,
                 )
 
-        def squares_of(s):
-            square(s, 1)
-            square(s, 0)
+        u_banks, squares, cubic, k2_rows, k_woven, k_mx = {}, {}, {}, {}, {}, {}
 
-        def make_cubic_factor(s):
-            cubic_factor[s] = work.tile([P, PACK, CHUNK], F32, name="cubic_factor")
-            affine(s, cubic_factor[s], gains["g3_mul"], gains["g3_add"])
+        def project(s, half):
+            chunk, e = divmod(s, F_PASSES)
+            x_codes, x_block_scales = x_mx[2 * chunk + half]
+            bank = psum.tile([P, SLOTS, P], F32, name="u", tag="u%d" % ((2 * s + half) % 4))
+            for t in range(SLOTS):
+                col = (e * SLOTS + t) * P
+                for a in range(K_PASSES):
+                    nc.tensor.matmul_mx(
+                        out=bank[:, t, :],
+                        lhsT=w_codes[a][:, 2 * col : 2 * (col + P)].bitcast(FP4X4),
+                        lhsT_scale=w_scale[:, a * F + col : a * F + col + P],
+                        rhs=x_codes[:, a * P : (a + 1) * P].bitcast(FP8X4),
+                        rhs_scale=x_block_scales[:, a * P : (a + 1) * P],
+                        start=(a == 0),
+                        stop=(a == K_PASSES - 1),
+                    )
+            u_banks[s, half] = bank
+
+        def square(s, halves):
+            squares[s] = work.tile([P, SLOTS, STEP_TOKENS], F32, name="squares")
+            for half in halves:
+                nc.scalar.activation(
+                    out=squares[s][:, :, half * P : (half + 1) * P], in_=u_banks[s, half][:], func=ACT.Square
+                )
+
+        def affine(s, rows, factor, offset):
+            e = s % F_PASSES
+            for t in range(SLOTS):
+                nc.scalar.activation(
+                    out=rows[:, t, :],
+                    in_=squares[s][:, t, :],
+                    func=ACT.Identity,
+                    scale=factor[:, e, t : t + 1],
+                    bias=offset[:, e, t : t + 1],
+                )
+
+        def make_cubic(s):
+            cubic[s] = work.tile([P, SLOTS, STEP_TOKENS], F32, name="cubic")
+            affine(s, cubic[s], g3_factor, g3_offset)
 
         def make_k2_rows(s):
-            k2_rows[s] = work.tile([P, PACK, CHUNK], BF16, name="k2_rows")
-            affine(s, k2_rows[s], gains["g2_mul"], gains["g2_add"])
+            k2_rows[s] = work.tile([P, SLOTS, STEP_TOKENS], BF16, name="k2_rows")
+            affine(s, k2_rows[s], g2_factor, g2_offset)
 
-        k_grouped, k_quant = {}, {}
-
-        slot_of = {0: 0, 2: 1, 1: 2}
-
-        def grouped(s, d):
-            if (s, d) not in k_grouped:
-                if d == 1 and 4 <= s <= 6:
-                    kg = work.tile([P, CHUNK * PACK], BF16, name="k2_late", align_bytes=64, bufs=1)[:]
+        def woven_k(s, d):
+            if (s, d) not in k_woven:
+                if d == K2 and X_STEPS <= s < LAST:
+                    flat = gpsimd_tile([P, STEP_TOKENS * SLOTS], "k2_woven")[:]
                 else:
-                    kg = stage(s)[:, slot_of[d], :]
-                k_grouped[s, d] = kg.rearrange("p (n t) -> p n t", t=PACK)
-            return k_grouped[s, d]
+                    flat = step_tile(s)[:, QUARTER[d], :]
+                k_woven[s, d] = flat.rearrange("p (n t) -> p n t", t=SLOTS)
+            return k_woven[s, d]
 
-        def quantize_stage(s, parts):
-            codes, plane = quantize("stage%d" % s, stage(s)[:, :parts, :].rearrange("p a w -> p (a w)"))
-            for d in range(T):
-                if slot_of[d] < parts:
-                    for h in range(2):
-                        cols = slice(slot_of[d] * CHUNK + h * P, slot_of[d] * CHUNK + (h + 1) * P)
-                        k_quant[s, d, h] = codes[:, cols], plane[:, cols]
-            if parts == 4:
-                cols = slice(3 * CHUNK, 4 * CHUNK)
-                x_codes[s + 4], x_planes[s + 4] = codes[:, cols], plane[:, cols]
-
-        def make_k1(s, h):
-            gf = s % F_PASSES
+        def make_k1(s, half):
+            e = s % F_PASSES
             nc.vector.tensor_tensor(
-                out=grouped(s, 0)[:, h * P : (h + 1) * P, :],
-                in0=u_banks[s, h][:].rearrange("p t n -> p n t"),
-                in1=gains["g1"][:, gf : gf + 1, :].to_broadcast([P, P, PACK]),
+                out=woven_k(s, K1)[:, half * P : (half + 1) * P, :],
+                in0=u_banks[s, half][:].rearrange("p t n -> p n t"),
+                in1=g1[:, e : e + 1, :].to_broadcast([P, P, SLOTS]),
                 op=ALU.mult,
             )
 
-        def make_k3(s, h):
-            cols = slice(h * P, (h + 1) * P)
+        def make_k3(s, half):
+            cols = slice(half * P, (half + 1) * P)
             nc.vector.tensor_tensor(
-                out=grouped(s, 2)[:, cols, :].rearrange("p (n i) t -> p n t i", i=2),
-                in0=u_banks[s, h][:].rearrange("p t (n i) -> p n t i", i=2),
-                in1=cubic_factor[s][:, :, cols].rearrange("p t (n i) -> p n t i", i=2),
+                out=woven_k(s, K3)[:, cols, :].rearrange("p (n i) t -> p n t i", i=2),
+                in0=u_banks[s, half][:].rearrange("p t (n i) -> p n t i", i=2),
+                in1=cubic[s][:, :, cols].rearrange("p t (n i) -> p n t i", i=2),
                 op=ALU.mult,
             )
 
-        def interleave(engine, dst, src):
-            if engine == "gpsimd":
-                src = src.rearrange("p t n -> p n t")
-                nc.gpsimd.tensor_scalar(out=dst, in0=src, scalar1=1.0, scalar2=0.0, op0=ALU.mult, op1=ALU.add)
-                return
-            dst = dst.rearrange("p (n i) t -> p n t i", i=4)
-            src = src.rearrange("p t (n i) -> p n t i", i=4)
-            if engine == "vector":
-                nc.vector.tensor_copy(out=dst, in_=src)
-            else:
-                nc.scalar.copy(out=dst, in_=src)
+        def make_k1_rows(s, half):
+            rows = keep.tile([P, SLOTS, P], BF16, name="k1_rows")
+            for t in range(SLOTS):
+                nc.scalar.activation(
+                    out=rows[:, t, :],
+                    in_=u_banks[s, half][:, t, :],
+                    func=ACT.Copy,
+                    scale=g1[:, s % F_PASSES, t : t + 1],
+                )
+            return rows
 
-        def make_k2(s, engine, cols=slice(0, CHUNK)):
-            interleave(engine, grouped(s, 1)[:, cols, :], k2_rows[s][:, :, cols])
+        def weave_on_gpsimd(woven, rows):
+            nc.gpsimd.tensor_scalar(
+                out=woven, in0=rows.rearrange("p t n -> p n t"), scalar1=1.0, scalar2=0.0, op0=ALU.mult, op1=ALU.add
+            )
 
-        k2_banks = {}
+        def weave_on_scalar(woven, rows):
+            nc.scalar.copy(
+                out=woven.rearrange("p (n i) t -> p n t i", i=4), in_=rows.rearrange("p t (n i) -> p n t i", i=4)
+            )
 
-        def weave_k2(s):
-            bank = psum.tile([P, CHUNK, PACK], BF16, name="weave", tag="acc%d" % (s % 2) if s < 4 else "turn0")
-            for h in range(2):
-                cols = slice(h * P, (h + 1) * P)
+        def weave_on_tensor(rows, tag):
+            tokens = rows.shape[2]
+            bank = psum.tile([P, tokens, SLOTS], BF16, name="weave", tag=tag)
+            for start in range(0, tokens, P):
+                cols = slice(start, start + P)
                 nc.tensor.matmul(
                     out=bank[:, cols, :].rearrange("p (n i) t -> p n t i", i=8),
                     lhsT=ident_bf[:],
-                    rhs=k2_rows[s][:, :, cols].rearrange("p t (n i) -> p n t i", i=8),
+                    rhs=rows[:, :, cols].rearrange("p t (n i) -> p n t i", i=8),
                     start=True,
                     stop=True,
                 )
-            k2_banks[s] = bank
+            return bank
 
-        def empty_k2(s):
-            nc.scalar.copy(out=grouped(s, 1), in_=k2_banks[s][:])
+        c_woven, c_mx = {}, {}
 
-        def quantize_k(s, d):
-            codes, plane = quantize("k%d_%d" % (d + 1, s), k_grouped[s, d].rearrange("p n t -> p (n t)"))
-            for h in range(2):
-                k_quant[s, d, h] = codes[:, h * P : (h + 1) * P], plane[:, h * P : (h + 1) * P]
-
-        c_grouped, c_quant = {}, {}
-
-        def group_c(m, engine, cols=slice(0, O)):
-            if m not in c_grouped:
-                c_grouped[m] = work.tile([P, O, PACK], BF16, name="c_grouped", align_bytes=64, bufs=1)
-            interleave(engine, c_grouped[m][:, cols, :], c_raw[m][:, :, cols])
+        def weave_c(m, weave, cols):
+            if m not in c_woven:
+                c_woven[m] = gpsimd_tile([P, O, SLOTS], "c_woven")
+            weave(c_woven[m][:, cols, :], c_rows[m][:, :, cols])
 
         def quantize_c(m):
-            c_quant[m] = quantize("c%d" % m, c_grouped[m][:].rearrange("p o t -> p (o t)"))
+            c_mx[m] = quantize("c%d" % m, c_woven[m][:].rearrange("p o t -> p (o t)"))
 
-        out_banks = {}
+        def note_k(s, d, codes, scales, start):
+            for half in range(2):
+                cols = slice(start + half * P, start + (half + 1) * P)
+                k_mx[s, d, half] = codes[:, cols], scales[:, cols]
 
-        def readout(i, gf, d):
-            j, h = divmod(i, 2)
-            first = i not in out_banks
-            if first:
-                out_banks[i] = psum.tile([P, O], F32, name="acc", tag=("acc%d" if j % 2 == 0 else "turn%d") % h)
-            k_codes, k_plane = k_quant[j * F_PASSES + gf, d, h]
-            c_codes, c_plane = c_quant[d * F_PASSES + gf]
-            nc.tensor.matmul_mx(
-                out=out_banks[i][:],
-                lhsT=k_codes.bitcast(FP8X4),
-                lhsT_scale=k_plane,
-                rhs=c_codes[:].bitcast(FP8X4),
-                rhs_scale=c_plane[:],
-                start=first,
-                stop=(gf == F_PASSES - 1 and d == 2),
-            )
+        def quantize_k(s, d):
+            codes, scales = quantize("k%d_%d" % (d + 1, s), woven_k(s, d).rearrange("p n t -> p (n t)"))
+            note_k(s, d, codes, scales, 0)
 
-        def readout_tile(i):
-            for gf in range(F_PASSES):
-                for d in range(T):
-                    readout(i, gf, d)
+        def quantize_step(s):
+            quarters = 4 if s < X_STEPS else 2
+            codes, scales = quantize("step%d" % s, step_tile(s)[:, :quarters, :].rearrange("p a w -> p (a w)"))
+            for d in (K1, K2, K3):
+                if QUARTER[d] < quarters:
+                    note_k(s, d, codes, scales, QUARTER[d] * STEP_TOKENS)
+            if s < X_STEPS:
+                cols = slice(X_QUARTER * STEP_TOKENS, (X_QUARTER + 1) * STEP_TOKENS)
+                x_mx[HEAD_TILES + s] = codes[:, cols], scales[:, cols]
+
+        sums, added = {}, {}
+
+        def read_out(tiles):
+            for i in tiles:
+                chunk, half = divmod(i, 2)
+                for m in range(C_PARTS):
+                    d, e = divmod(m, F_PASSES)
+                    k_key = (chunk * F_PASSES + e, d, half)
+                    if m in added.setdefault(i, []) or m not in c_mx or k_key not in k_mx:
+                        continue
+                    if i not in sums:
+                        sums[i] = psum.tile([P, O], F32, name="sums", tag=SUM_BANKS[i % 4])
+                    added[i].append(m)
+                    nc.tensor.matmul_mx(
+                        out=sums[i][:],
+                        lhsT=k_mx[k_key][0].bitcast(FP8X4),
+                        lhsT_scale=k_mx[k_key][1],
+                        rhs=c_mx[m][0][:].bitcast(FP8X4),
+                        rhs_scale=c_mx[m][1][:],
+                        start=(len(added[i]) == 1),
+                        stop=(len(added[i]) == C_PARTS),
+                    )
 
         def finish(i):
-            res = keep.tile([P, O], F32, name="result%d" % i)
-            nc.vector.tensor_tensor(out=res[:], in0=out_banks[i][:], in1=bias[:], op=ALU.add)
-            nc.sync.dma_start(out=out[i * P : (i + 1) * P, :], in_=res[:])
-
-        WOVEN = 5
-
-        passes = [(gf, d) for d in range(T) for gf in range(F_PASSES)]
-
-        def read_passes(tiles, which):
-            for i in tiles:
-                for gf, d in which:
-                    readout(i, gf, d)
+            result = keep.tile([P, O], F32, name="result%d" % i)
+            nc.vector.tensor_tensor(out=result[:], in0=sums[i][:], in1=bias[:], op=ALU.add)
+            nc.sync.dma_start(out=out[i * P : (i + 1) * P, :], in_=result[:])
 
         widen_x(0)
-        turn_x(0)
+        turn_first_tile()
         widen_x(1)
-        turn_gains()
-        order_w(0)
-        order_w(1)
-        scale_x(0)
+        g_bank = turn_gains()
+        scale_first_tile()
         turn_x(1)
+        w_codes = [order_w_codes(a) for a in range(K_PASSES)]
+        x_mx[0] = quantize("x0", x_woven[0])
+        w_scale = order_w_scales()
         widen_x(2)
         widen_x(3)
         turn_x(2)
-        order_w_scales()
-        quantize_x(0)
         project(0, 0)
-        scale_x(1)
-        quantize_x(1)
+        scale_x(1, gpsimd_tile([P, D], "c_woven")[:])
+        g1 = gain("g1", g_bank, 0, 1.0)
+        g3_factor = gain("g3_factor", g_bank, 2, 1.0 / math.sqrt(6.0))
+        g3_offset = gain("g3_offset", g_bank, 2, -3.0 / math.sqrt(6.0))
+        g2_factor = gain("g2_factor", g_bank, 1, 1.0 / math.sqrt(2.0))
+        g2_offset = gain("g2_offset", g_bank, 1, -1.0 / math.sqrt(2.0))
+        x_mx[1] = quantize("x1", x_woven[1])
         project(0, 1)
         turn_x(3)
         project(1, 0)
         project(1, 1)
-        group_c(0, "gpsimd")
-        scale_x(2)
-        scale_gains()
+        weave_c(0, weave_on_gpsimd, slice(0, O))
+        x23_woven = keep.tile([P, 2, D], BF16, name="x23_woven", align_bytes=64)
+        scale_x(2, x23_woven[:, 0, :])
         widen_x(4)
         turn_x(4)
         widen_x(5)
-        square(0, 0)
-        square(0, 1)
-        make_cubic_factor(0)
+        square(0, (0, 1))
+        make_cubic(0)
         make_k2_rows(0)
-        weave_k2(0)
-        squares_of(1)
+        k2_bank = weave_on_tensor(k2_rows[0][:], WEAVE_BANK)
+        square(1, (1, 0))
         make_k1(0, 0)
-        scale_x(3)
+        scale_x(3, x23_woven[:, 1, :])
         make_k1(0, 1)
         quantize_c(0)
-        quantize_x23()
-        for s in range(STEPS - 1):
-            if s < 4:
-                group_c(s + 1, "gpsimd")
-            elif s == 4:
-                group_c(5, "gpsimd", slice(0, 320))
+        x23_codes, x23_scales = quantize("x23", x23_woven[:].rearrange("p a w -> p (a w)"))
+        for i in (2, 3):
+            cols = slice((i - 2) * K_PASSES * P, (i - 1) * K_PASSES * P)
+            x_mx[i] = x23_codes[:, cols], x23_scales[:, cols]
+
+        last_c = C_PARTS - 1
+        for s in range(LAST):
+            if s + 1 < last_c:
+                weave_c(s + 1, weave_on_gpsimd, slice(0, O))
+            elif s + 1 == last_c:
+                weave_c(last_c, weave_on_gpsimd, slice(0, LAST_C_SPLIT))
             else:
-                make_k2(s, "gpsimd")
-            if s + 5 < ROW_TILES:
-                turn_x(s + 5)
+                weave_on_gpsimd(woven_k(s, K2), k2_rows[s][:])
+
+            if HEAD_TILES + s + 1 < TILES:
+                turn_x(HEAD_TILES + s + 1)
             make_k3(s, 0)
+            if s + 1 == LAST:
+                k1_bank = weave_on_tensor(last_k1_rows[:], "u%d" % (2 * s % 4))
+                read_out([5])
             make_k3(s, 1)
             if s + 2 < STEPS:
                 project(s + 2, 0)
                 project(s + 2, 1)
-            if s == 3:
-                read_passes((0, 1), passes[:4])
-            if s == 4:
-                read_passes((0, 1), passes[4:5])
-            if s == 5:
-                read_passes((3,), passes)
-            if s == 4:
-                group_c(5, "scalar", slice(320, O))
-            if s + 6 < ROW_TILES:
-                widen_x(s + 6)
-            if s < 2:
-                empty_k2(s)
-            make_cubic_factor(s + 1)
-            if 2 <= s < WOVEN:
-                empty_k2(s)
+            if 2 <= s <= last_c:
+                read_out(range(s - 1))
+
+            other_work = HEAD_TILES + s + 2 < TILES or s + 1 == last_c
+            if s + 1 == last_c:
+                weave_c(last_c, weave_on_scalar, slice(LAST_C_SPLIT, O))
+            if HEAD_TILES + s + 2 < TILES:
+                widen_x(HEAD_TILES + s + 2)
+            if other_work:
+                nc.scalar.copy(out=woven_k(s, K2), in_=k2_bank[:])
+            make_cubic(s + 1)
+            if s < TENSOR_K2_STEPS and not other_work:
+                nc.scalar.copy(out=woven_k(s, K2), in_=k2_bank[:])
             make_k2_rows(s + 1)
-            if s + 1 < WOVEN:
-                weave_k2(s + 1)
+            if s + 1 == LAST:
+                nc.scalar.copy(out=woven_k(LAST, K1)[:, :P, :], in_=k1_bank[:])
+            if s + 1 < TENSOR_K2_STEPS:
+                k2_bank = weave_on_tensor(k2_rows[s + 1][:], WEAVE_BANK)
+
             make_k1(s + 1, 1)
-            if s + 4 < ROW_TILES:
-                scale_x(s + 4)
-            make_k1(s + 1, 0)
-            if s + 2 < STEPS:
-                squares_of(s + 2)
-            if s >= 5:
-                finish(2 * (s - 5) + 1)
-                finish(2 * (s - 5))
-            if s < 5:
+            if s < X_STEPS:
+                scale_x(HEAD_TILES + s, step_tile(s)[:, X_QUARTER, :])
+            if s + 1 < LAST:
+                make_k1(s + 1, 0)
+                square(s + 2, (1, 0))
+            if s + 2 == LAST:
+                last_k1_rows = make_k1_rows(LAST, 0)
+            if s >= last_c:
+                finish(2 * (s - last_c) + 1)
+                finish(2 * (s - last_c))
+
+            if s + 1 <= last_c:
                 quantize_c(s + 1)
-            if s >= 4:
-                quantize_k(s, 1)
-            quantize_stage(s, 4 if s < 4 else 2)
-            if s == 6:
-                quantize_k(7, 0)
-            if s == 4:
-                read_passes((0, 1), passes[5:])
-                read_passes((2,), passes)
-            if s == 5:
-                read_passes((4, 5), passes)
-            if s == 6:
-                for one in [(0, 1), (0, 0), (0, 2), (1, 0)]:
-                    read_passes((6, 7), [one])
-        make_k2(7, "scalar")
-        make_k3(7, 0)
-        make_k3(7, 1)
-        quantize_k(7, 1)
-        quantize_k(7, 2)
-        read_passes((6, 7), [(1, 1), (1, 2)])
-        for i in range(4, ROW_TILES):
+            if s >= X_STEPS:
+                quantize_k(s, K2)
+            if s + 1 == LAST:
+                read_out([6, 7])
+            quantize_step(s)
+            if s + 1 == last_c:
+                read_out([0, 1, 2])
+            if s == last_c:
+                read_out([4])
+            if s + 1 == LAST:
+                read_out([6, 7])
+                quantize_k(LAST, K1)
+                read_out([6, 7])
+
+        weave_on_scalar(woven_k(LAST, K2), k2_rows[LAST][:])
+        make_k3(LAST, 0)
+        make_k3(LAST, 1)
+        quantize_k(LAST, K2)
+        quantize_k(LAST, K3)
+        read_out([6, 7])
+        for i in range(4, TILES):
             finish(i)

import math
from contextlib import ExitStack

import concourse.mybir as mybir
from concourse.masks import make_identity

N, D, F, O, T = 1024, 1024, 1024, 512, 3
FLOPS = 2 * N * D * F + T * 2 * N * F * O

F32 = mybir.dt.float32
BF16 = mybir.dt.bfloat16
I32 = mybir.dt.int32
U32 = mybir.dt.uint32
U8 = mybir.dt.uint8
FP8 = mybir.dt.float8_e4m3fn
FP8X4 = mybir.dt.float8_e4m3fn_x4
FP4X4 = mybir.dt.float4_e2m1fn_x4
ALU = mybir.AluOpType
ACT = mybir.ActivationFunctionType

P = 128
SLOTS = 4
PASS = P * SLOTS
K_PASSES = D // PASS
F_PASSES = F // PASS
RUN = 8
BLOCKS = PASS // 32
TILES = N // P
STEP_TOKENS = 2 * P
STEPS = (N // STEP_TOKENS) * F_PASSES
LAST = STEPS - 1
C_PARTS = T * F_PASSES

K1, K2, K3 = 0, 1, 2
QUARTER = {K1: 0, K3: 1, K2: 2}
X_QUARTER = 3
HEAD_TILES = 4
X_STEPS = TILES - HEAD_TILES

TENSOR_K2_STEPS = C_PARTS - 1
LAST_C_SPLIT = 320

TURN_BANKS = ("side0", "side1")
WEAVE_BANK = "side2"
SPARE_BANK = "side3"
SUM_BANKS = (SPARE_BANK, TURN_BANKS[0], TURN_BANKS[1], WEAVE_BANK)


def tile_hermitechaosridgeexpansiondegreethree_w4_kernel(
    tc, x_bytes, x_scale, w_words, w_scales, g, c, b, out
):
    nc = tc.nc
    with ExitStack() as ctx:
        keep = ctx.enter_context(tc.tile_pool(name="keep", bufs=1))
        work = ctx.enter_context(tc.tile_pool(name="work", bufs=2))
        psum = ctx.enter_context(tc.psum_pool(name="psum", bufs=1))
        ctx.enter_context(tc.manual_schedule())

        g_raw = keep.tile([C_PARTS, PASS], BF16, name="g_raw")
        nc.gpsimd.dma_start(out=g_raw[:], in_=g.rearrange("d (e f) -> (d e) f", e=F_PASSES))
        ident = keep.tile([P, P], F32, name="ident")
        make_identity(nc, ident[:])
        ident_bf = keep.tile([P, P], BF16, name="ident_bf")
        nc.gpsimd.tensor_copy(out=ident_bf[:], in_=ident[:])
        w_scale_raw = keep.tile([P, K_PASSES * F // 4], I32, name="w_scale_raw")
        nc.vector.memset(w_scale_raw[:], 0)
        g_rows = keep.tile([P, SLOTS, P], F32, name="g_rows")
        nc.vector.memset(g_rows[:], 0.0)

        x_raw, c_rows = {}, {}

        def load_x(i):
            x_raw[i] = keep.tile([P, D], U8, name="x_raw%d" % i)
            nc.sync.dma_start(out=x_raw[i][:], in_=x_bytes[i * P : (i + 1) * P, :])

        def load_c(m):
            d, e = divmod(m, F_PASSES)
            c_rows[m] = keep.tile([P, SLOTS, O], BF16, name="c_rows%d" % m)
            by_slot = c[d, e * PASS : (e + 1) * PASS, :].rearrange("(q t r) o -> t q r o", t=SLOTS, r=RUN)
            for t in range(SLOTS):
                nc.sync.dma_start(out=c_rows[m][:, t, :], in_=by_slot[t])

        load_x(0)
        x_scales = keep.tile([P, K_PASSES, SLOTS], F32, name="x_scales")
        nc.sync.dma_start(out=x_scales[:], in_=x_scale.rearrange("o (a p t) -> p (o a) t", p=P, t=SLOTS))
        load_x(1)
        w_raw = keep.tile([P, K_PASSES, F // 2], I32, name="w_raw")
        nc.sync.dma_start(out=w_raw[:], in_=w_words.rearrange("a p n -> p a n").bitcast(I32))
        for j in range(4):
            nc.sync.dma_start(
                out=w_scale_raw[32 * j : 32 * j + 4, :].rearrange("r (a n) -> r a n", a=K_PASSES),
                in_=w_scales[:, 4 * j : 4 * j + 4, :].rearrange("a r n -> r a n").bitcast(I32),
            )
        for i in (2, 3, 4):
            load_x(i)
        load_c(0)
        load_x(5)
        load_x(6)
        load_c(1)
        load_x(7)
        for m in range(2, C_PARTS):
            load_c(m)
        bias = keep.tile([P, O], BF16, name="bias")
        nc.sync.dma_start(out=bias[:], in_=b.partition_broadcast(P))

        def turn_gains():
            nc.vector.tensor_copy(
                out=g_rows[0:C_PARTS].rearrange("m t (q r) -> m t q r", r=RUN),
                in_=g_raw[:].rearrange("m (q t r) -> m t q r", t=SLOTS, r=RUN),
            )
            bank = psum.tile([P, SLOTS, P], F32, name="g_bank", tag=WEAVE_BANK)
            for t in range(SLOTS):
                nc.tensor.transpose(bank[:, t, :], g_rows[:, t, :], ident[:])
            return bank

        def gain(name, bank, d, factor):
            scaled = keep.tile([P, F_PASSES, SLOTS], F32, name=name)
            src = bank[:, :, d * F_PASSES : (d + 1) * F_PASSES].rearrange("p t e -> p e t")
            nc.vector.tensor_scalar(out=scaled[:], in0=src, scalar1=factor, scalar2=None, op0=ALU.mult)
            return scaled

        def order_w_codes(a):
            codes = keep.tile([P, 2 * F], U8, name="w_codes%d" % a, align_bytes=64)
            nc.vector.tensor_copy(
                out=codes[:].bitcast(I32).rearrange("p (e t q w) -> p e t q w", e=F_PASSES, t=SLOTS, w=4),
                in_=w_raw[:, a, :].rearrange("p (e q t w) -> p e t q w", e=F_PASSES, t=SLOTS, w=4),
            )
            return codes

        def order_w_scales():
            scales = keep.tile([P, K_PASSES * F], U8, name="w_scale", align_bytes=64)
            nc.vector.tensor_copy(
                out=scales[:].bitcast(I32).rearrange("p (ae t q w) -> p ae t q w", t=SLOTS, q=BLOCKS, w=2),
                in_=w_scale_raw[:].rearrange("p (ae q t w) -> p ae t q w", t=SLOTS, q=BLOCKS, w=2),
            )
            return scales

        def quantize(name, woven):
            width = woven.shape[1] // SLOTS
            codes = keep.tile([P, width], U32, name=name + "_codes", align_bytes=64)
            scales = keep.tile([P, width], U8, name=name + "_scales", align_bytes=64)
            nc.vector.quantize_mx(out=codes[:].bitcast(FP8X4), scales=scales[:], in_=woven)
            return codes, scales

        step_tiles = {}

        def step_tile(s):
            if s not in step_tiles:
                step_tiles[s] = work.tile([P, 4, STEP_TOKENS * SLOTS], BF16, name="step_tile", align_bytes=64, bufs=3)
            return step_tiles[s]

        def gpsimd_tile(shape, tag):
            return work.tile(shape, BF16, name=tag, align_bytes=64, bufs=1)

        x_wide, x_turned, x_woven, x_mx = {}, {}, {}, {}

        def widen_x(i):
            x_wide[i] = work.tile([P, D], BF16, name="x_wide", bufs=6)
            start = PASS if i == 0 else 0
            if start:
                nc.vector.tensor_copy(out=x_wide[i][:, :start], in_=x_raw[i][:, :start].bitcast(FP8))
            nc.scalar.activation(out=x_wide[i][:, start:], in_=x_raw[i][:, start:].bitcast(FP8), func=ACT.Copy)

        def turn_pass(i, a, dst):
            words = x_wide[i][:].bitcast(F32)
            for j in range(2):
                nc.tensor.transpose(dst[:, j, :], words[:, 256 * a + j : 256 * (a + 1) : 2], ident[:])

        def turn_x(i):
            x_turned[i] = psum.tile([P, 2, K_PASSES, P], F32, name="x_turned", tag=TURN_BANKS[i % 2])
            for a in range(K_PASSES):
                turn_pass(i, a, x_turned[i][:, :, a, :])

        def scale_x(i, woven):
            nc.vector.tensor_tensor(
                out=woven.rearrange("p (a n j h) -> p a n j h", a=K_PASSES, j=2, h=2),
                in0=x_turned[i][:].bitcast(BF16).rearrange("p j a (n h) -> p a n j h", h=2),
                in1=x_scales[:].rearrange("p a (o j h) -> p a o j h", o=1, h=2).to_broadcast([P, K_PASSES, P, 2, 2]),
                op=ALU.mult,
            )
            x_woven[i] = woven

        def turn_first_tile():
            for a, tag in enumerate((TURN_BANKS[0], SPARE_BANK)):
                x_turned[0, a] = psum.tile([P, 2, P], F32, name="x_turned", tag=tag)
                turn_pass(0, a, x_turned[0, a][:])

        def scale_first_tile():
            x_woven[0] = keep.tile([P, D], BF16, name="x0_woven", align_bytes=64)[:]
            for a in range(K_PASSES):
                nc.vector.tensor_tensor(
                    out=x_woven[0][:, a * PASS : (a + 1) * PASS].rearrange("p (n j h) -> p n j h", j=2, h=2),
                    in0=x_turned[0, a][:].bitcast(BF16).rearrange("p j (n h) -> p n j h", h=2),
                    in1=x_scales[:, a : a + 1, :].rearrange("p o (j h) -> p o j h", h=2).to_broadcast([P, P, 2, 2]),
                    op=ALU.mult,
                )

        u_banks, squares, cubic, k2_rows, k_woven, k_mx = {}, {}, {}, {}, {}, {}

        def project(s, half):
            chunk, e = divmod(s, F_PASSES)
            x_codes, x_block_scales = x_mx[2 * chunk + half]
            bank = psum.tile([P, SLOTS, P], F32, name="u", tag="u%d" % ((2 * s + half) % 4))
            for t in range(SLOTS):
                col = (e * SLOTS + t) * P
                for a in range(K_PASSES):
                    nc.tensor.matmul_mx(
                        out=bank[:, t, :],
                        lhsT=w_codes[a][:, 2 * col : 2 * (col + P)].bitcast(FP4X4),
                        lhsT_scale=w_scale[:, a * F + col : a * F + col + P],
                        rhs=x_codes[:, a * P : (a + 1) * P].bitcast(FP8X4),
                        rhs_scale=x_block_scales[:, a * P : (a + 1) * P],
                        start=(a == 0),
                        stop=(a == K_PASSES - 1),
                    )
            u_banks[s, half] = bank

        def square(s, halves):
            squares[s] = work.tile([P, SLOTS, STEP_TOKENS], F32, name="squares")
            for half in halves:
                nc.scalar.activation(
                    out=squares[s][:, :, half * P : (half + 1) * P], in_=u_banks[s, half][:], func=ACT.Square
                )

        def affine(s, rows, factor, offset):
            e = s % F_PASSES
            for t in range(SLOTS):
                nc.scalar.activation(
                    out=rows[:, t, :],
                    in_=squares[s][:, t, :],
                    func=ACT.Identity,
                    scale=factor[:, e, t : t + 1],
                    bias=offset[:, e, t : t + 1],
                )

        def make_cubic(s):
            cubic[s] = work.tile([P, SLOTS, STEP_TOKENS], F32, name="cubic")
            affine(s, cubic[s], g3_factor, g3_offset)

        def make_k2_rows(s):
            k2_rows[s] = work.tile([P, SLOTS, STEP_TOKENS], BF16, name="k2_rows")
            affine(s, k2_rows[s], g2_factor, g2_offset)

        def woven_k(s, d):
            if (s, d) not in k_woven:
                if d == K2 and X_STEPS <= s < LAST:
                    flat = gpsimd_tile([P, STEP_TOKENS * SLOTS], "k2_woven")[:]
                else:
                    flat = step_tile(s)[:, QUARTER[d], :]
                k_woven[s, d] = flat.rearrange("p (n t) -> p n t", t=SLOTS)
            return k_woven[s, d]

        def make_k1(s, half):
            e = s % F_PASSES
            nc.vector.tensor_tensor(
                out=woven_k(s, K1)[:, half * P : (half + 1) * P, :],
                in0=u_banks[s, half][:].rearrange("p t n -> p n t"),
                in1=g1[:, e : e + 1, :].to_broadcast([P, P, SLOTS]),
                op=ALU.mult,
            )

        def make_k3(s, half):
            cols = slice(half * P, (half + 1) * P)
            nc.vector.tensor_tensor(
                out=woven_k(s, K3)[:, cols, :].rearrange("p (n i) t -> p n t i", i=2),
                in0=u_banks[s, half][:].rearrange("p t (n i) -> p n t i", i=2),
                in1=cubic[s][:, :, cols].rearrange("p t (n i) -> p n t i", i=2),
                op=ALU.mult,
            )

        def make_k1_rows(s, half):
            rows = keep.tile([P, SLOTS, P], BF16, name="k1_rows")
            for t in range(SLOTS):
                nc.scalar.activation(
                    out=rows[:, t, :],
                    in_=u_banks[s, half][:, t, :],
                    func=ACT.Copy,
                    scale=g1[:, s % F_PASSES, t : t + 1],
                )
            return rows

        def weave_on_gpsimd(woven, rows):
            nc.gpsimd.tensor_scalar(
                out=woven, in0=rows.rearrange("p t n -> p n t"), scalar1=1.0, scalar2=0.0, op0=ALU.mult, op1=ALU.add
            )

        def weave_on_scalar(woven, rows):
            nc.scalar.copy(
                out=woven.rearrange("p (n i) t -> p n t i", i=4), in_=rows.rearrange("p t (n i) -> p n t i", i=4)
            )

        def weave_on_tensor(rows, tag):
            tokens = rows.shape[2]
            bank = psum.tile([P, tokens, SLOTS], BF16, name="weave", tag=tag)
            for start in range(0, tokens, P):
                cols = slice(start, start + P)
                nc.tensor.matmul(
                    out=bank[:, cols, :].rearrange("p (n i) t -> p n t i", i=8),
                    lhsT=ident_bf[:],
                    rhs=rows[:, :, cols].rearrange("p t (n i) -> p n t i", i=8),
                    start=True,
                    stop=True,
                )
            return bank

        c_woven, c_mx = {}, {}

        def weave_c(m, weave, cols):
            if m not in c_woven:
                c_woven[m] = gpsimd_tile([P, O, SLOTS], "c_woven")
            weave(c_woven[m][:, cols, :], c_rows[m][:, :, cols])

        def quantize_c(m):
            c_mx[m] = quantize("c%d" % m, c_woven[m][:].rearrange("p o t -> p (o t)"))

        def note_k(s, d, codes, scales, start):
            for half in range(2):
                cols = slice(start + half * P, start + (half + 1) * P)
                k_mx[s, d, half] = codes[:, cols], scales[:, cols]

        def quantize_k(s, d):
            codes, scales = quantize("k%d_%d" % (d + 1, s), woven_k(s, d).rearrange("p n t -> p (n t)"))
            note_k(s, d, codes, scales, 0)

        def quantize_step(s):
            quarters = 4 if s < X_STEPS else 2
            codes, scales = quantize("step%d" % s, step_tile(s)[:, :quarters, :].rearrange("p a w -> p (a w)"))
            for d in (K1, K2, K3):
                if QUARTER[d] < quarters:
                    note_k(s, d, codes, scales, QUARTER[d] * STEP_TOKENS)
            if s < X_STEPS:
                cols = slice(X_QUARTER * STEP_TOKENS, (X_QUARTER + 1) * STEP_TOKENS)
                x_mx[HEAD_TILES + s] = codes[:, cols], scales[:, cols]

        sums, added = {}, {}

        def read_out(tiles):
            for i in tiles:
                chunk, half = divmod(i, 2)
                for m in range(C_PARTS):
                    d, e = divmod(m, F_PASSES)
                    k_key = (chunk * F_PASSES + e, d, half)
                    if m in added.setdefault(i, []) or m not in c_mx or k_key not in k_mx:
                        continue
                    if i not in sums:
                        sums[i] = psum.tile([P, O], F32, name="sums", tag=SUM_BANKS[i % 4])
                    added[i].append(m)
                    nc.tensor.matmul_mx(
                        out=sums[i][:],
                        lhsT=k_mx[k_key][0].bitcast(FP8X4),
                        lhsT_scale=k_mx[k_key][1],
                        rhs=c_mx[m][0][:].bitcast(FP8X4),
                        rhs_scale=c_mx[m][1][:],
                        start=(len(added[i]) == 1),
                        stop=(len(added[i]) == C_PARTS),
                    )

        def finish(i):
            result = keep.tile([P, O], F32, name="result%d" % i)
            nc.vector.tensor_tensor(out=result[:], in0=sums[i][:], in1=bias[:], op=ALU.add)
            nc.sync.dma_start(out=out[i * P : (i + 1) * P, :], in_=result[:])

        widen_x(0)
        turn_first_tile()
        widen_x(1)
        g_bank = turn_gains()
        scale_first_tile()
        turn_x(1)
        w_codes = [order_w_codes(a) for a in range(K_PASSES)]
        x_mx[0] = quantize("x0", x_woven[0])
        w_scale = order_w_scales()
        widen_x(2)
        widen_x(3)
        turn_x(2)
        project(0, 0)
        scale_x(1, gpsimd_tile([P, D], "c_woven")[:])
        g1 = gain("g1", g_bank, 0, 1.0)
        g3_factor = gain("g3_factor", g_bank, 2, 1.0 / math.sqrt(6.0))
        g3_offset = gain("g3_offset", g_bank, 2, -3.0 / math.sqrt(6.0))
        g2_factor = gain("g2_factor", g_bank, 1, 1.0 / math.sqrt(2.0))
        g2_offset = gain("g2_offset", g_bank, 1, -1.0 / math.sqrt(2.0))
        x_mx[1] = quantize("x1", x_woven[1])
        project(0, 1)
        turn_x(3)
        project(1, 0)
        project(1, 1)
        weave_c(0, weave_on_gpsimd, slice(0, O))
        x23_woven = keep.tile([P, 2, D], BF16, name="x23_woven", align_bytes=64)
        scale_x(2, x23_woven[:, 0, :])
        widen_x(4)
        turn_x(4)
        widen_x(5)
        square(0, (0, 1))
        make_cubic(0)
        make_k2_rows(0)
        k2_bank = weave_on_tensor(k2_rows[0][:], WEAVE_BANK)
        square(1, (1, 0))
        make_k1(0, 0)
        scale_x(3, x23_woven[:, 1, :])
        make_k1(0, 1)
        quantize_c(0)
        x23_codes, x23_scales = quantize("x23", x23_woven[:].rearrange("p a w -> p (a w)"))
        for i in (2, 3):
            cols = slice((i - 2) * K_PASSES * P, (i - 1) * K_PASSES * P)
            x_mx[i] = x23_codes[:, cols], x23_scales[:, cols]

        last_c = C_PARTS - 1
        for s in range(LAST):
            if s + 1 < last_c:
                weave_c(s + 1, weave_on_gpsimd, slice(0, O))
            elif s + 1 == last_c:
                weave_c(last_c, weave_on_gpsimd, slice(0, LAST_C_SPLIT))
            else:
                weave_on_gpsimd(woven_k(s, K2), k2_rows[s][:])

            if HEAD_TILES + s + 1 < TILES:
                turn_x(HEAD_TILES + s + 1)
            make_k3(s, 0)
            if s + 1 == LAST:
                k1_bank = weave_on_tensor(last_k1_rows[:], "u%d" % (2 * s % 4))
                read_out([5])
            make_k3(s, 1)
            if s + 2 < STEPS:
                project(s + 2, 0)
                project(s + 2, 1)
            if 2 <= s <= last_c:
                read_out(range(s - 1))

            other_work = HEAD_TILES + s + 2 < TILES or s + 1 == last_c
            if s + 1 == last_c:
                weave_c(last_c, weave_on_scalar, slice(LAST_C_SPLIT, O))
            if HEAD_TILES + s + 2 < TILES:
                widen_x(HEAD_TILES + s + 2)
            if other_work:
                nc.scalar.copy(out=woven_k(s, K2), in_=k2_bank[:])
            make_cubic(s + 1)
            if s < TENSOR_K2_STEPS and not other_work:
                nc.scalar.copy(out=woven_k(s, K2), in_=k2_bank[:])
            make_k2_rows(s + 1)
            if s + 1 == LAST:
                nc.scalar.copy(out=woven_k(LAST, K1)[:, :P, :], in_=k1_bank[:])
            if s + 1 < TENSOR_K2_STEPS:
                k2_bank = weave_on_tensor(k2_rows[s + 1][:], WEAVE_BANK)

            make_k1(s + 1, 1)
            if s < X_STEPS:
                scale_x(HEAD_TILES + s, step_tile(s)[:, X_QUARTER, :])
            if s + 1 < LAST:
                make_k1(s + 1, 0)
                square(s + 2, (1, 0))
            if s + 2 == LAST:
                last_k1_rows = make_k1_rows(LAST, 0)
            if s >= last_c:
                finish(2 * (s - last_c) + 1)
                finish(2 * (s - last_c))

            if s + 1 <= last_c:
                quantize_c(s + 1)
            if s >= X_STEPS:
                quantize_k(s, K2)
            if s + 1 == LAST:
                read_out([6, 7])
            quantize_step(s)
            if s + 1 == last_c:
                read_out([0, 1, 2])
            if s == last_c:
                read_out([4])
            if s + 1 == LAST:
                read_out([6, 7])
                quantize_k(LAST, K1)
                read_out([6, 7])

        weave_on_scalar(woven_k(LAST, K2), k2_rows[LAST][:])
        make_k3(LAST, 0)
        make_k3(LAST, 1)
        quantize_k(LAST, K2)
        quantize_k(LAST, K3)
        read_out([6, 7])
        for i in range(4, TILES):
            finish(i)
